import numpy as np
import ml_dtypes


def mxq(x, axis, fmt="e4m3"):
    dtype, down = {"e4m3": (ml_dtypes.float8_e4m3fn, 7), "e5m2": (ml_dtypes.float8_e5m2, 14)}[fmt]
    v = np.moveaxis(np.asarray(x, np.float32).astype(ml_dtypes.bfloat16).astype(np.float64), axis, -1)
    blocks = v.reshape(v.shape[:-1] + (-1, 32))
    amax = np.abs(blocks).max(-1, keepdims=True)
    byte = np.maximum(np.where(amax > 0, np.frexp(amax)[1] - 1 + 127, 0) - down, 1)
    scale = np.exp2(byte - 127.0)
    codes = (blocks / scale).astype(np.float32).astype(dtype).astype(np.float64)
    return np.moveaxis((codes * scale).reshape(v.shape), -1, axis)


WIDE = False


def mx_kscale(k):
    if not WIDE:
        return np.ones(k)
    levels = np.array([10, -10, 5, -5, 0])
    if k % 512:
        return np.exp2(np.random.permutation(np.resize(levels, k // 32))).repeat(32)
    a = np.empty((k // 512, 16))
    for p in range(k // 512):
        a[p, :8] = np.random.permutation(np.resize(levels, 8))
        for g in range(8):
            far = levels[np.abs(levels - a[p, g]) >= 10]
            a[p, g + 8] = far[np.random.randint(len(far))]
    return np.exp2(a.ravel()).repeat(32)


def f64(x):
    return np.asarray(x).astype(np.float64)


def striped(idx):
    return np.tile(idx.reshape(-1, 16).T, (8, 1)).astype(np.uint16)


def unstriped(offs):
    return offs[:16].T.reshape(-1).astype(np.int64)


E2M1 = np.array([0.0, 0.5, 1.0, 1.5, 2.0, 3.0, 4.0, 6.0, -0.0, -0.5, -1.0, -1.5, -2.0, -3.0, -4.0, -6.0])


def pack_weight(w, fmt):
    k, n = w.shape
    w = f64(np.asarray(w, np.float32).astype(ml_dtypes.bfloat16)).reshape(k // 32, 32, n)
    amax = np.abs(w).max(1)
    if fmt == "e4m3":
        byte = np.frexp(amax)[1] - 1 + 127 - 7
    else:
        mant, ex = np.frexp(amax / 6.0)
        byte = np.where(mant > 0.5, ex, ex - 1) + 127
    byte = np.clip(np.where(amax > 0, byte, 1), 1, 254)
    scaled = (w * np.exp2(127.0 - byte)[:, None, :]).reshape(k, n).astype(np.float32)
    by_word = np.ascontiguousarray(scaled.reshape(k // 512, 128, 4, n).transpose(0, 1, 3, 2))
    if fmt == "e4m3":
        words = by_word.astype(ml_dtypes.float8_e4m3fn).view(np.uint8)
    else:
        c = by_word.astype(ml_dtypes.float4_e2m1fn).view(np.uint8) & 0xF
        words = (c[..., 0::2] | (c[..., 1::2] << 4)).reshape(k // 512, 128, 2 * n)
    return np.ascontiguousarray(words), np.ascontiguousarray(byte.astype(np.uint8).reshape(k // 512, 16, n))


def unpack_weight(words, scales, fmt):
    g, _, n = scales.shape
    words = np.ascontiguousarray(words).reshape(g, 128, n, -1)
    if fmt == "e4m3":
        vals = words.view(ml_dtypes.float8_e4m3fn).astype(np.float64)
    else:
        nib = np.empty((g, 128, n, 4), np.uint8)
        nib[..., 0::2] = words & 0xF
        nib[..., 1::2] = words >> 4
        vals = E2M1[nib]
    vals = vals * np.repeat(np.exp2(scales.astype(np.float64) - 127.0), 8, axis=1)[..., None]
    return vals.transpose(0, 1, 3, 2).reshape(g * 512, n)


def gelu(v):
    return 0.5 * v * (1.0 + np.tanh(np.sqrt(2.0 / np.pi) * (v + 0.044715 * v**3)))


K, H, N, T, S = 1024, 1024, 512, 2048, 1024

def setup_inputs():
    n = np.random.standard_normal
    s = mx_kscale(K)[:, None]
    u = mx_kscale(H)[:, None]
    tab_words, tab_scales = pack_weight(n((K, T)) * s, "e4m3")
    w1_words, w1_scales = pack_weight(n((K, H)) / np.sqrt(K) / s * u.T, "e2m1")
    w2 = (1.5 * n((K, H)) / np.sqrt(K) / s).astype(np.float32)
    w3 = (1.5 * n((H, N)) / np.sqrt(H) / u).astype(np.float32)
    gT = np.abs(n((N, T))).astype(np.float32)
    offs = striped(np.random.permutation(T)[:S])
    return {"tab_words": tab_words, "tab_scales": tab_scales,
            "w1_words": w1_words, "w1_scales": w1_scales,
            "w2": w2, "w3": w3, "gT": gT, "offs": offs}

def reference(tab_words, tab_scales, w1_words, w1_scales, w2, w3, gT, offs):
    v = unpack_weight(tab_words, tab_scales, "e4m3")[:, unstriped(offs)]
    w1 = unpack_weight(w1_words, w1_scales, "e2m1")
    a = w1.T @ v
    b = mxq(f64(w2), 0, "e4m3").T @ v
    h = a / (1.0 + np.abs(b))
    y = mxq(f64(w3), 0, "e4m3").T @ mxq(h, 0, "e4m3")
    g = f64(gT)[:, unstriped(offs)]
    new = np.maximum(g + y, 0.0)
    out = f64(gT).copy()
    out[:, unstriped(offs)] = new
    return out

@@ -1,0 +1,253 @@
+from contextlib import ExitStack
+
+import concourse.mybir as mybir
+from concourse.masks import make_identity
+
+K, H, N, T, S = 1024, 1024, 512, 2048, 1024
+FLOPS = 2 * S * (2 * K * H + H * N)
+
+F32 = mybir.dt.float32
+BF16 = mybir.dt.bfloat16
+I32 = mybir.dt.int32
+U32 = mybir.dt.uint32
+U16 = mybir.dt.uint16
+U8 = mybir.dt.uint8
+E4M3 = mybir.dt.float8_e4m3fn_x4
+E2M1 = mybir.dt.float4_e2m1fn_x4
+ACT = mybir.ActivationFunctionType
+ALU = mybir.AluOpType
+
+P = 128
+PASS = 512
+CAST_ON_VECTOR = (2, 3, 4, 5)
+UNITS = [(jt, rh) for c in range(4) for rh in range(2) for jt in (2 * c, 2 * c + 1)]
+REST = 4
+LEAD = 4
+W3 = (2, 3)
+WIDTH = 256
+
+
+def tile_list_cap_voxel_update_kernel(
+    tc, tab_words, tab_scales, w1_words, w1_scales, w2, w3, gT, offs, out
+):
+    nc = tc.nc
+    with ExitStack() as ctx:
+        keep = ctx.enter_context(tc.tile_pool(name="keep", bufs=1))
+        ring = ctx.enter_context(tc.tile_pool(name="ring", bufs=3))
+        psum = ctx.enter_context(tc.psum_pool(name="psum", bufs=1))
+
+        offsets = keep.tile([P, S // 16], U16, name="offsets")
+        nc.sync.dma_start(offsets[:], offs)
+
+        tab_plane = keep.tile([P, T], U8, name="tab_plane", align_bytes=64)
+        moved_plane = keep.tile([P, S], U8, name="moved_plane", align_bytes=64)
+        w1_plane = keep.tile([P, 2, H], U8, name="w1_plane", align_bytes=64)
+        nc.vector.memset(tab_plane[:].bitcast(I32), 0)
+        nc.vector.memset(w1_plane[:].bitcast(I32), 0)
+        nc.vector.memset(moved_plane[:].bitcast(I32), 0)
+        tab, raws = {}, {}
+
+        def load_table(a):
+            tab[a] = keep.tile([P, T], U32, name="tab%d" % a)
+            nc.sync.dma_start(
+                tab[a][:].bitcast(I32), tab_words[a].rearrange("p t i -> p (t i)").bitcast(I32)
+            )
+
+        blocks = [w2[PASS * a : PASS * (a + 1), PASS * rh : PASS * (rh + 1)] for rh in range(2) for a in range(2)]
+        blocks = blocks + [w3[PASS * b : PASS * (b + 1), :] for b in range(2)]
+
+        def load_weight(c):
+            raws[c] = keep.tile([P, 4, PASS], F32, name="raw%d" % c)
+            nc.sync.dma_start(raws[c][:], blocks[c].rearrange("(p i) c -> p i c", i=4))
+
+        load_table(0)
+        for q in range(4):
+            nc.sync.dma_start(
+                tab_plane[32 * q : 32 * q + 8, :].bitcast(I32),
+                tab_scales[:, 4 * q : 4 * q + 4, :].bitcast(I32),
+            )
+        load_weight(0)
+        load_weight(1)
+        load_table(1)
+        load_weight(2)
+        load_weight(3)
+        w1_codes = keep.tile([P, 2, 2 * H], U8, name="w1_codes", align_bytes=64)
+        nc.sync.dma_start(
+            w1_codes[:].bitcast(I32), w1_words.rearrange("a p c -> p a c").bitcast(I32)
+        )
+        for q in range(4):
+            nc.sync.dma_start(
+                w1_plane[32 * q : 32 * q + 4, :, :].bitcast(I32),
+                w1_scales[:, 4 * q : 4 * q + 4, :].rearrange("a r c -> r a c").bitcast(I32),
+            )
+        load_weight(4)
+        load_weight(5)
+
+        volume = []
+        for n in range(N // P):
+            rows = keep.tile([P, T], F32, name="volume%d" % n)
+            nc.sync.dma_start(rows[:], gT[P * n : P * (n + 1), :])
+            volume.append(rows)
+
+        ident = keep.tile([P, P], F32, name="ident")
+        make_identity(nc, ident[:])
+
+        v_codes = {}
+
+        def pick_codes(a, part):
+            j0, j1 = ((0, WIDTH), (WIDTH, S))[part]
+            v_codes[a, part] = keep.tile([P, j1 - j0], U32, name="v_codes%d%d" % (a, part), align_bytes=64)
+            nc.vector.tensor_copy(v_codes[a, part][:], tab[a][:].indirect(offsets[:, j0 // 16 : j1 // 16]))
+
+        v_plane = keep.tile([P, S], U8, name="v_plane", align_bytes=64)
+
+        def pick_scales():
+            nc.vector.tensor_copy(v_plane[:], tab_plane[:].indirect(offsets[:]))
+            nc.gpsimd.dma_start(moved_plane[: P - 4, :].bitcast(I32), v_plane[4:, :].bitcast(I32))
+
+        w_codes, w_scales = {}, {}
+
+        def quantize_weight(c):
+            grouped = ring.tile([P, PASS, 4], BF16, name="grouped", align_bytes=64)
+            dst = grouped[:].rearrange("p (c k) i -> p c i k", k=4)
+            src = raws[c][:].rearrange("p i (c k) -> p c i k", k=4)
+            if c in CAST_ON_VECTOR:
+                nc.vector.tensor_copy(dst, src)
+            else:
+                nc.scalar.copy(dst, src)
+            w_codes[c] = keep.tile([P, PASS], U32, name="w_codes%d" % c, align_bytes=64)
+            w_scales[c] = keep.tile([P, PASS], U8, name="w_scales%d" % c, align_bytes=64)
+            nc.vector.quantize_mx(
+                out=w_codes[c][:].bitcast(E4M3),
+                scales=w_scales[c][:],
+                in_=grouped[:].rearrange("p c i -> p (c i)"),
+            )
+
+        def in_word_order(bank):
+            return bank[:].rearrange("j (p u e) -> j u p e", u=2, e=2)
+
+        h_rows = {}
+
+        def damped_drive(jt, rh):
+            js = slice(P * jt, P * (jt + 1))
+            half = min(P * jt // WIDTH, 1)
+            jh = slice(P * jt - WIDTH * half, P * (jt + 1) - WIDTH * half)
+            damping = psum.tile([P, PASS], F32, name="damping", bufs=2)
+            for a in range(2):
+                nc.tensor.matmul_mx(
+                    out=damping[:],
+                    lhsT=v_codes[a, half][:, jh].bitcast(E4M3),
+                    lhsT_scale=v_plane[4 * a :, js],
+                    rhs=w_codes[2 * rh + a][:].bitcast(E4M3),
+                    rhs_scale=w_scales[2 * rh + a][:],
+                    start=(a == 0),
+                    stop=(a == 1),
+                )
+            drive = psum.tile([P, PASS], F32, name="drive", bufs=3)
+            for a in range(2):
+                nc.tensor.matmul_mx(
+                    out=drive[:],
+                    lhsT=v_codes[a, half][:, jh].bitcast(E4M3),
+                    lhsT_scale=(v_plane, moved_plane)[a][:, js],
+                    rhs=w1_codes[:, a, 2 * PASS * rh : 2 * PASS * (rh + 1)].bitcast(E2M1),
+                    rhs_scale=w1_plane[:, a, PASS * rh : PASS * (rh + 1)],
+                    start=(a == 0),
+                    stop=(a == 1),
+                )
+            size = ring.tile([P, PASS], F32, name="size")
+            nc.scalar.activation(
+                size[:].rearrange("j (u p e) -> j u p e", u=2, e=2), in_word_order(damping), ACT.Abs
+            )
+            root = ring.tile([P, PASS], F32, name="root")
+            nc.scalar.activation(root[:], size[:], ACT.Abs_reciprocal_sqrt, bias=1.0)
+            factor = ring.tile([P, PASS], F32, name="factor", bufs=4)
+            nc.scalar.activation(factor[:], root[:], ACT.Square)
+            h_rows[jt, rh] = ring.tile([P, PASS], BF16, name="h_rows", bufs=8)
+            nc.vector.tensor_tensor(
+                h_rows[jt, rh][:].rearrange("j (u p e) -> j u p e", u=2, e=2),
+                in_word_order(drive),
+                factor[:].rearrange("j (u p e) -> j u p e", u=2, e=2),
+                ALU.mult,
+            )
+
+        h_grouped = {}
+
+        def turn(jt):
+            c, j0 = divmod(P * jt, WIDTH)
+            if j0 == 0:
+                h_grouped[c] = ring.tile([P, 2, WIDTH, 2], F32, name="h_grouped", align_bytes=64, bufs=2)
+            turned = psum.tile([P, 2, 2, P], F32, name="turned")
+            for rh in range(2):
+                words = h_rows[jt, rh][:].bitcast(F32)
+                for u in range(2):
+                    nc.tensor.transpose(turned[:, rh, u, :], words[:, P * u : P * (u + 1)], ident[:])
+            nc.scalar.copy(
+                h_grouped[c][:, :, j0 : j0 + P, :], turned[:].rearrange("p b u j -> p b j u")
+            )
+
+        h_codes, h_scales = {}, {}
+
+        def quantize_h(c):
+            h_codes[c] = keep.tile([P, 2, WIDTH], U32, name="h_codes%d" % c, align_bytes=64)
+            h_scales[c] = keep.tile([P, 2, WIDTH], U8, name="h_scales%d" % c, align_bytes=64)
+            nc.vector.quantize_mx(
+                out=h_codes[c][:].rearrange("p b j -> p (b j)").bitcast(E4M3),
+                scales=h_scales[c][:].rearrange("p b j -> p (b j)"),
+                in_=h_grouped[c][:].rearrange("p b j u -> p (b j u)").bitcast(BF16),
+            )
+
+        def listed(c, n):
+            return volume[n][:].indirect(offsets[:, WIDTH // 16 * c : WIDTH // 16 * (c + 1)])
+
+        summed = {}
+
+        def add_change(c, n):
+            ns = slice(P * n, P * (n + 1))
+            bank = psum.tile([P, WIDTH], F32, name="change_bank", bufs=2)
+            for b in range(2):
+                nc.tensor.matmul_mx(
+                    out=bank[:],
+                    lhsT=w_codes[4 + b][:, ns].bitcast(E4M3),
+                    lhsT_scale=w_scales[4 + b][:, ns],
+                    rhs=h_codes[c][:, b, :].bitcast(E4M3),
+                    rhs_scale=h_scales[c][:, b, :],
+                    start=(b == 0),
+                    stop=(b == 1),
+                )
+            change = ring.tile([P, WIDTH], F32, name="change")
+            nc.scalar.copy(change[:], bank[:])
+            summed[c, n] = ring.tile([P, WIDTH], F32, name="summed")
+            nc.vector.tensor_tensor(summed[c, n][:], listed(c, n), change[:], ALU.add)
+
+        def put_back(c, n):
+            new = ring.tile([P, WIDTH], F32, name="new")
+            nc.scalar.activation(new[:], summed[c, n][:], ACT.Relu)
+            nc.vector.tensor_copy(listed(c, n), new[:])
+            if c == S // WIDTH - 1:
+                nc.sync.dma_start(out[P * n : P * (n + 1), :], volume[n][:])
+
+        pick_codes(0, 0)
+        pick_scales()
+        quantize_weight(0)
+        pick_codes(1, 0)
+        for c in range(1, 4):
+            quantize_weight(c)
+        units = UNITS
+        jobs = [(c, n) for c in range(S // WIDTH) for n in range(N // P)]
+        for step in range(LEAD + len(jobs) + 1):
+            if step < len(units):
+                if step == REST:
+                    pick_codes(0, 1)
+                    pick_codes(1, 1)
+                damped_drive(*units[step])
+            if step in W3:
+                quantize_weight(4 + W3.index(step))
+            if 1 <= step <= len(units) and units[step - 1][1] == 1:
+                jt = units[step - 1][0]
+                turn(jt)
+                if jt % 2 == 1:
+                    quantize_h(jt // 2)
+            if LEAD <= step < LEAD + len(jobs):
+                add_change(*jobs[step - LEAD])
+            if step > LEAD:
+                put_back(*jobs[step - LEAD - 1])

@@ -19,12 +19,21 @@ ALU = mybir.AluOpType
 
 P = 128
 PASS = 512
-CAST_ON_VECTOR = (2, 3, 4, 5)
-UNITS = [(jt, rh) for c in range(4) for rh in range(2) for jt in (2 * c, 2 * c + 1)]
-REST = 4
-LEAD = 4
-W3 = (2, 3)
-WIDTH = 256
+ON_VECTOR = (0, 256, 512, 512, 0, 512)
+CHUNKS = (512, 512)
+RING = 5
+JOB0 = 11
+JOBSTEP = 3
+W3 = (4, 5)
+PICKS = (4, 5, 6, 7)
+REST = 2
+FIRST = 256
+LOADS = "t0 s c0 c1 t1 c2 c3 w c4 c5 g0 g1 g2 g3"
+UNITS = [(jt, rh) for c in range(2) for rh in range(2) for jt in range(4 * c, 4 * c + 4)]
+TL = 2
+WARM = 1
+FB = 5
+PW = 1024
 
 
 def tile_list_cap_voxel_update_kernel(
@@ -41,10 +50,17 @@ def tile_list_cap_voxel_update_kernel(
 
         tab_plane = keep.tile([P, T], U8, name="tab_plane", align_bytes=64)
         moved_plane = keep.tile([P, S], U8, name="moved_plane", align_bytes=64)
-        w1_plane = keep.tile([P, 2, H], U8, name="w1_plane", align_bytes=64)
-        nc.vector.memset(tab_plane[:].bitcast(I32), 0)
-        nc.vector.memset(w1_plane[:].bitcast(I32), 0)
         nc.vector.memset(moved_plane[:].bitcast(I32), 0)
+        w1_plane = keep.tile([P, 2, H], U8, name="w1_plane", align_bytes=64)
+        nc.gpsimd.memset(tab_plane[:].bitcast(I32), 0)
+        nc.gpsimd.memset(w1_plane[:].bitcast(I32), 0)
+        for q in range(4):
+            nc.gpsimd.dma_start(
+                w1_plane[32 * q : 32 * q + 4, :, :].bitcast(I32),
+                w1_scales[:, 4 * q : 4 * q + 4, :].rearrange("a r c -> r a c").bitcast(I32),
+            )
+
+
         tab, raws = {}, {}
 
         def load_table(a):
@@ -60,34 +76,32 @@ def tile_list_cap_voxel_update_kernel(
             raws[c] = keep.tile([P, 4, PASS], F32, name="raw%d" % c)
             nc.sync.dma_start(raws[c][:], blocks[c].rearrange("(p i) c -> p i c", i=4))
 
-        load_table(0)
-        for q in range(4):
-            nc.sync.dma_start(
-                tab_plane[32 * q : 32 * q + 8, :].bitcast(I32),
-                tab_scales[:, 4 * q : 4 * q + 4, :].bitcast(I32),
-            )
-        load_weight(0)
-        load_weight(1)
-        load_table(1)
-        load_weight(2)
-        load_weight(3)
         w1_codes = keep.tile([P, 2, 2 * H], U8, name="w1_codes", align_bytes=64)
-        nc.sync.dma_start(
-            w1_codes[:].bitcast(I32), w1_words.rearrange("a p c -> p a c").bitcast(I32)
-        )
-        for q in range(4):
-            nc.sync.dma_start(
-                w1_plane[32 * q : 32 * q + 4, :, :].bitcast(I32),
-                w1_scales[:, 4 * q : 4 * q + 4, :].rearrange("a r c -> r a c").bitcast(I32),
-            )
-        load_weight(4)
-        load_weight(5)
+        volume = {}
+        for item in LOADS.split():
+            if item[0] == "t":
+                load_table(int(item[1]))
+            if item[0] == "c":
+                load_weight(int(item[1]))
+            if item[0] == "g":
+                n = int(item[1])
+                volume[n] = keep.tile([P, T], F32, name="volume%d" % n)
+                nc.sync.dma_start(volume[n][:], gT[P * n : P * (n + 1), :])
+            if item == "s":
+                for q in range(4):
+                    nc.sync.dma_start(
+                        tab_plane[32 * q : 32 * q + 8, :].bitcast(I32),
+                        tab_scales[:, 4 * q : 4 * q + 4, :].bitcast(I32),
+                    )
+            if item == "w":
+                nc.sync.dma_start(
+                    w1_codes[:].bitcast(I32), w1_words.rearrange("a p c -> p a c").bitcast(I32)
+                )
 
-        volume = []
-        for n in range(N // P):
-            rows = keep.tile([P, T], F32, name="volume%d" % n)
-            nc.sync.dma_start(rows[:], gT[P * n : P * (n + 1), :])
-            volume.append(rows)
+        if WARM:
+            warm = keep.tile([P, 2], F32, name="warm")
+            nc.vector.memset(warm[:, :1], 1.0)
+            nc.scalar.activation(warm[:, 1:], warm[:, :1], ACT.Abs_reciprocal_sqrt)
 
         ident = keep.tile([P, P], F32, name="ident")
         make_identity(nc, ident[:])
@@ -95,7 +109,7 @@ def tile_list_cap_voxel_update_kernel(
         v_codes = {}
 
         def pick_codes(a, part):
-            j0, j1 = ((0, WIDTH), (WIDTH, S))[part]
+            j0, j1 = ((0, FIRST), (FIRST, S))[part]
             v_codes[a, part] = keep.tile([P, j1 - j0], U32, name="v_codes%d%d" % (a, part), align_bytes=64)
             nc.vector.tensor_copy(v_codes[a, part][:], tab[a][:].indirect(offsets[:, j0 // 16 : j1 // 16]))
 
@@ -103,7 +117,7 @@ def tile_list_cap_voxel_update_kernel(
 
         def pick_scales():
             nc.vector.tensor_copy(v_plane[:], tab_plane[:].indirect(offsets[:]))
-            nc.gpsimd.dma_start(moved_plane[: P - 4, :].bitcast(I32), v_plane[4:, :].bitcast(I32))
+            nc.gpsimd.dma_start(moved_plane[:112, :].bitcast(I32), v_plane[4:116, :].bitcast(I32))
 
         w_codes, w_scales = {}, {}
 
@@ -111,10 +125,11 @@ def tile_list_cap_voxel_update_kernel(
             grouped = ring.tile([P, PASS, 4], BF16, name="grouped", align_bytes=64)
             dst = grouped[:].rearrange("p (c k) i -> p c i k", k=4)
             src = raws[c][:].rearrange("p i (c k) -> p c i k", k=4)
-            if c in CAST_ON_VECTOR:
-                nc.vector.tensor_copy(dst, src)
-            else:
-                nc.scalar.copy(dst, src)
+            cut = ON_VECTOR[c] // 4
+            if cut > 0:
+                nc.vector.tensor_copy(dst[:, :cut], src[:, :cut])
+            if cut < PASS // 4:
+                nc.scalar.copy(dst[:, cut:], src[:, cut:])
             w_codes[c] = keep.tile([P, PASS], U32, name="w_codes%d" % c, align_bytes=64)
             w_scales[c] = keep.tile([P, PASS], U8, name="w_scales%d" % c, align_bytes=64)
             nc.vector.quantize_mx(
@@ -123,6 +138,13 @@ def tile_list_cap_voxel_update_kernel(
                 in_=grouped[:].rearrange("p c i -> p (c i)"),
             )
 
+        acc_count = [0]
+
+        def acc_bank():
+            bank = psum.tile([P, PASS], F32, name="acc%d" % (acc_count[0] % RING))
+            acc_count[0] = acc_count[0] + 1
+            return bank
+
         def in_word_order(bank):
             return bank[:].rearrange("j (p u e) -> j u p e", u=2, e=2)
 
@@ -130,9 +152,9 @@ def tile_list_cap_voxel_update_kernel(
 
         def damped_drive(jt, rh):
             js = slice(P * jt, P * (jt + 1))
-            half = min(P * jt // WIDTH, 1)
-            jh = slice(P * jt - WIDTH * half, P * (jt + 1) - WIDTH * half)
-            damping = psum.tile([P, PASS], F32, name="damping", bufs=2)
+            half = min(P * jt // FIRST, 1)
+            jh = slice(P * jt - FIRST * half, P * (jt + 1) - FIRST * half)
+            damping = psum.tile([P, PASS], F32, name="damping", bufs=8 - RING)
             for a in range(2):
                 nc.tensor.matmul_mx(
                     out=damping[:],
@@ -143,7 +165,7 @@ def tile_list_cap_voxel_update_kernel(
                     start=(a == 0),
                     stop=(a == 1),
                 )
-            drive = psum.tile([P, PASS], F32, name="drive", bufs=3)
+            drive = acc_bank()
             for a in range(2):
                 nc.tensor.matmul_mx(
                     out=drive[:],
@@ -160,7 +182,7 @@ def tile_list_cap_voxel_update_kernel(
             )
             root = ring.tile([P, PASS], F32, name="root")
             nc.scalar.activation(root[:], size[:], ACT.Abs_reciprocal_sqrt, bias=1.0)
-            factor = ring.tile([P, PASS], F32, name="factor", bufs=4)
+            factor = ring.tile([P, PASS], F32, name="factor", bufs=FB)
             nc.scalar.activation(factor[:], root[:], ACT.Square)
             h_rows[jt, rh] = ring.tile([P, PASS], BF16, name="h_rows", bufs=8)
             nc.vector.tensor_tensor(
@@ -170,26 +192,32 @@ def tile_list_cap_voxel_update_kernel(
                 ALU.mult,
             )
 
+        starts = [sum(CHUNKS[:c]) for c in range(len(CHUNKS) + 1)]
+
+        def chunk_of(jt):
+            c = max(k for k in range(len(CHUNKS)) if starts[k] <= P * jt)
+            return c, P * jt - starts[c]
+
         h_grouped = {}
 
         def turn(jt):
-            c, j0 = divmod(P * jt, WIDTH)
+            c, j0 = chunk_of(jt)
             if j0 == 0:
-                h_grouped[c] = ring.tile([P, 2, WIDTH, 2], F32, name="h_grouped", align_bytes=64, bufs=2)
-            turned = psum.tile([P, 2, 2, P], F32, name="turned")
+                h_grouped[c] = ring.tile([P, 2, CHUNKS[c], 2], F32, name="h_grouped", align_bytes=64, bufs=2)
+            turned = acc_bank()[:].rearrange("p (b u j) -> p b u j", b=2, u=2)
             for rh in range(2):
                 words = h_rows[jt, rh][:].bitcast(F32)
                 for u in range(2):
                     nc.tensor.transpose(turned[:, rh, u, :], words[:, P * u : P * (u + 1)], ident[:])
             nc.scalar.copy(
-                h_grouped[c][:, :, j0 : j0 + P, :], turned[:].rearrange("p b u j -> p b j u")
+                h_grouped[c][:, :, j0 : j0 + P, :], turned.rearrange("p b u j -> p b j u")
             )
 
         h_codes, h_scales = {}, {}
 
         def quantize_h(c):
-            h_codes[c] = keep.tile([P, 2, WIDTH], U32, name="h_codes%d" % c, align_bytes=64)
-            h_scales[c] = keep.tile([P, 2, WIDTH], U8, name="h_scales%d" % c, align_bytes=64)
+            h_codes[c] = keep.tile([P, 2, CHUNKS[c]], U32, name="h_codes%d" % c, align_bytes=64)
+            h_scales[c] = keep.tile([P, 2, CHUNKS[c]], U8, name="h_scales%d" % c, align_bytes=64)
             nc.vector.quantize_mx(
                 out=h_codes[c][:].rearrange("p b j -> p (b j)").bitcast(E4M3),
                 scales=h_scales[c][:].rearrange("p b j -> p (b j)"),
@@ -197,16 +225,24 @@ def tile_list_cap_voxel_update_kernel(
             )
 
         def listed(c, n):
-            return volume[n][:].indirect(offsets[:, WIDTH // 16 * c : WIDTH // 16 * (c + 1)])
+            return volume[n][:].indirect(offsets[:, starts[c] // 16 : starts[c + 1] // 16])
 
-        summed = {}
+        picked = {}
 
-        def add_change(c, n):
+        def pick_old(n):
+            picked[n] = keep.tile([P, S], F32, name="picked%d" % n)
+            for j0 in range(0, S, PW):
+                nc.vector.tensor_copy(picked[n][:, j0 : j0 + PW], volume[n][:].indirect(offsets[:, j0 // 16 : (j0 + PW) // 16]))
+
+        steps_made = {}
+
+        def first_half(c, n):
             ns = slice(P * n, P * (n + 1))
-            bank = psum.tile([P, WIDTH], F32, name="change_bank", bufs=2)
+            bank = acc_bank()[:, : CHUNKS[c]]
+            steps_made[c, n] = ring.tile([P, CHUNKS[c]], F32, name="new", bufs=4)
             for b in range(2):
                 nc.tensor.matmul_mx(
-                    out=bank[:],
+                    out=bank,
                     lhsT=w_codes[4 + b][:, ns].bitcast(E4M3),
                     lhsT_scale=w_scales[4 + b][:, ns],
                     rhs=h_codes[c][:, b, :].bitcast(E4M3),
@@ -214,16 +250,13 @@ def tile_list_cap_voxel_update_kernel(
                     start=(b == 0),
                     stop=(b == 1),
                 )
-            change = ring.tile([P, WIDTH], F32, name="change")
-            nc.scalar.copy(change[:], bank[:])
-            summed[c, n] = ring.tile([P, WIDTH], F32, name="summed")
-            nc.vector.tensor_tensor(summed[c, n][:], listed(c, n), change[:], ALU.add)
+            old = picked[n][:, starts[c] : starts[c + 1]]
+            nc.vector.scalar_tensor_tensor(steps_made[c, n][:], old, -1.0, bank, op0=ALU.mult, op1=ALU.max)
 
-        def put_back(c, n):
-            new = ring.tile([P, WIDTH], F32, name="new")
-            nc.scalar.activation(new[:], summed[c, n][:], ACT.Relu)
-            nc.vector.tensor_copy(listed(c, n), new[:])
-            if c == S // WIDTH - 1:
+        def second_half(c, n):
+            old = picked[n][:, starts[c] : starts[c + 1]]
+            nc.vector.tensor_tensor(listed(c, n), old, steps_made[c, n][:], ALU.add)
+            if c == len(CHUNKS) - 1:
                 nc.sync.dma_start(out[P * n : P * (n + 1), :], volume[n][:])
 
         pick_codes(0, 0)
@@ -233,21 +266,27 @@ def tile_list_cap_voxel_update_kernel(
         for c in range(1, 4):
             quantize_weight(c)
         units = UNITS
-        jobs = [(c, n) for c in range(S // WIDTH) for n in range(N // P)]
-        for step in range(LEAD + len(jobs) + 1):
+        jobs = [(c, n) for c in range(len(CHUNKS)) for n in range(N // P)]
+        job_at = {JOB0 + JOBSTEP * k: job for k, job in enumerate(jobs)}
+        last = None
+        for step in range(max(job_at) + 2):
             if step < len(units):
-                if step == REST:
+                if step == REST and FIRST < S:
                     pick_codes(0, 1)
                     pick_codes(1, 1)
                 damped_drive(*units[step])
             if step in W3:
                 quantize_weight(4 + W3.index(step))
-            if 1 <= step <= len(units) and units[step - 1][1] == 1:
-                jt = units[step - 1][0]
+            if TL <= step < len(units) + TL and units[step - TL][1] == 1:
+                jt = units[step - TL][0]
                 turn(jt)
-                if jt % 2 == 1:
-                    quantize_h(jt // 2)
-            if LEAD <= step < LEAD + len(jobs):
-                add_change(*jobs[step - LEAD])
-            if step > LEAD:
-                put_back(*jobs[step - LEAD - 1])
+                c, j0 = chunk_of(jt)
+                if j0 + P == CHUNKS[c]:
+                    quantize_h(c)
+            if step in PICKS:
+                pick_old(PICKS.index(step))
+            if step in job_at:
+                first_half(*job_at[step])
+            if last:
+                second_half(*last)
+            last = job_at.get(step)

@@ -19,20 +19,24 @@ ALU = mybir.AluOpType
 
 P = 128
 PASS = 512
-ON_VECTOR = (0, 256, 512, 512, 0, 512)
-CHUNKS = (512, 512)
-RING = 5
-JOB0 = 11
-JOBSTEP = 3
+ON_VECTOR = (0, 0, 0, 512, 512, 0)
+CHUNKS = (256, 256, 512)
+RING = 4
+JOB0 = 10
+JOBSTEP = 2
 W3 = (4, 5)
 PICKS = (4, 5, 6, 7)
-REST = 2
-FIRST = 256
-LOADS = "t0 s c0 c1 t1 c2 c3 w c4 c5 g0 g1 g2 g3"
-UNITS = [(jt, rh) for c in range(2) for rh in range(2) for jt in range(4 * c, 4 * c + 4)]
-TL = 2
+REST = 0
+FIRST = 1024
+LOADS = "t0 s t1 c0 c1 c2 c3 w g0 c4 c5 g1 g2 g3"
+UNITS = [(jt, rh) for c in range(4) for rh in range(2) for jt in (2 * c, 2 * c + 1)]
+TL = 4
 WARM = 1
-FB = 5
+L = 2
+R1 = 6
+R2 = 2
+JOBS = (7, 8, 9, 10, 13, 15, 18, 19)
+FB = 8
 PW = 1024
 
 
@@ -48,18 +52,10 @@ def tile_list_cap_voxel_update_kernel(
         offsets = keep.tile([P, S // 16], U16, name="offsets")
         nc.sync.dma_start(offsets[:], offs)
 
-        tab_plane = keep.tile([P, T], U8, name="tab_plane", align_bytes=64)
-        moved_plane = keep.tile([P, S], U8, name="moved_plane", align_bytes=64)
-        nc.vector.memset(moved_plane[:].bitcast(I32), 0)
+        tab_plane = keep.tile([P, 2, T], U8, name="tab_plane", align_bytes=64)
         w1_plane = keep.tile([P, 2, H], U8, name="w1_plane", align_bytes=64)
         nc.gpsimd.memset(tab_plane[:].bitcast(I32), 0)
-        nc.gpsimd.memset(w1_plane[:].bitcast(I32), 0)
-        for q in range(4):
-            nc.gpsimd.dma_start(
-                w1_plane[32 * q : 32 * q + 4, :, :].bitcast(I32),
-                w1_scales[:, 4 * q : 4 * q + 4, :].rearrange("a r c -> r a c").bitcast(I32),
-            )
-
+        nc.vector.memset(w1_plane[:].bitcast(I32), 0)
 
         tab, raws = {}, {}
 
@@ -90,13 +86,18 @@ def tile_list_cap_voxel_update_kernel(
             if item == "s":
                 for q in range(4):
                     nc.sync.dma_start(
-                        tab_plane[32 * q : 32 * q + 8, :].bitcast(I32),
-                        tab_scales[:, 4 * q : 4 * q + 4, :].bitcast(I32),
+                        tab_plane[32 * q : 32 * q + 4, :, :].bitcast(I32),
+                        tab_scales[:, 4 * q : 4 * q + 4, :].rearrange("a r t -> r a t").bitcast(I32),
                     )
             if item == "w":
                 nc.sync.dma_start(
                     w1_codes[:].bitcast(I32), w1_words.rearrange("a p c -> p a c").bitcast(I32)
                 )
+                for q in range(4):
+                    nc.sync.dma_start(
+                        w1_plane[32 * q : 32 * q + 4, :, :].bitcast(I32),
+                        w1_scales[:, 4 * q : 4 * q + 4, :].rearrange("a r c -> r a c").bitcast(I32),
+                    )
 
         if WARM:
             warm = keep.tile([P, 2], F32, name="warm")
@@ -113,11 +114,11 @@ def tile_list_cap_voxel_update_kernel(
             v_codes[a, part] = keep.tile([P, j1 - j0], U32, name="v_codes%d%d" % (a, part), align_bytes=64)
             nc.vector.tensor_copy(v_codes[a, part][:], tab[a][:].indirect(offsets[:, j0 // 16 : j1 // 16]))
 
-        v_plane = keep.tile([P, S], U8, name="v_plane", align_bytes=64)
+        v_scales = {}
 
-        def pick_scales():
-            nc.vector.tensor_copy(v_plane[:], tab_plane[:].indirect(offsets[:]))
-            nc.gpsimd.dma_start(moved_plane[:112, :].bitcast(I32), v_plane[4:116, :].bitcast(I32))
+        def pick_scales(a):
+            v_scales[a] = keep.tile([P, S], U8, name="v_scales%d" % a, align_bytes=64)
+            nc.vector.tensor_copy(v_scales[a][:], tab_plane[:, a, :].indirect(offsets[:]))
 
         w_codes, w_scales = {}, {}
 
@@ -138,11 +139,11 @@ def tile_list_cap_voxel_update_kernel(
                 in_=grouped[:].rearrange("p c i -> p (c i)"),
             )
 
-        acc_count = [0]
+        taken = {"first": 0, "second": 0}
 
-        def acc_bank():
-            bank = psum.tile([P, PASS], F32, name="acc%d" % (acc_count[0] % RING))
-            acc_count[0] = acc_count[0] + 1
+        def next_bank(stage, depth):
+            bank = psum.tile([P, PASS], F32, name="%s%d" % (stage, taken[stage] % depth))
+            taken[stage] = taken[stage] + 1
             return bank
 
         def in_word_order(bank):
@@ -150,29 +151,23 @@ def tile_list_cap_voxel_update_kernel(
 
         h_rows = {}
 
-        def damped_drive(jt, rh):
-            js = slice(P * jt, P * (jt + 1))
-            half = min(P * jt // FIRST, 1)
-            jh = slice(P * jt - FIRST * half, P * (jt + 1) - FIRST * half)
-            damping = psum.tile([P, PASS], F32, name="damping", bufs=8 - RING)
+        factors = {}
+
+        def table_columns(a, jt):
+            part = min(P * jt // FIRST, 1)
+            codes = v_codes[a, part][:, P * jt - FIRST * part : P * (jt + 1) - FIRST * part]
+            return codes.bitcast(E4M3), v_scales[a][:, P * jt : P * (jt + 1)]
+
+        def damp(jt, rh):
+            damping = next_bank("first", R1)
             for a in range(2):
+                codes, scales = table_columns(a, jt)
                 nc.tensor.matmul_mx(
                     out=damping[:],
-                    lhsT=v_codes[a, half][:, jh].bitcast(E4M3),
-                    lhsT_scale=v_plane[4 * a :, js],
+                    lhsT=codes,
+                    lhsT_scale=scales,
                     rhs=w_codes[2 * rh + a][:].bitcast(E4M3),
                     rhs_scale=w_scales[2 * rh + a][:],
-                    start=(a == 0),
-                    stop=(a == 1),
-                )
-            drive = acc_bank()
-            for a in range(2):
-                nc.tensor.matmul_mx(
-                    out=drive[:],
-                    lhsT=v_codes[a, half][:, jh].bitcast(E4M3),
-                    lhsT_scale=(v_plane, moved_plane)[a][:, js],
-                    rhs=w1_codes[:, a, 2 * PASS * rh : 2 * PASS * (rh + 1)].bitcast(E2M1),
-                    rhs_scale=w1_plane[:, a, PASS * rh : PASS * (rh + 1)],
                     start=(a == 0),
                     stop=(a == 1),
                 )
@@ -182,13 +177,27 @@ def tile_list_cap_voxel_update_kernel(
             )
             root = ring.tile([P, PASS], F32, name="root")
             nc.scalar.activation(root[:], size[:], ACT.Abs_reciprocal_sqrt, bias=1.0)
-            factor = ring.tile([P, PASS], F32, name="factor", bufs=FB)
-            nc.scalar.activation(factor[:], root[:], ACT.Square)
-            h_rows[jt, rh] = ring.tile([P, PASS], BF16, name="h_rows", bufs=8)
+            factors[jt, rh] = ring.tile([P, PASS], F32, name="factor", bufs=FB)
+            nc.scalar.activation(factors[jt, rh][:], root[:], ACT.Square)
+
+        def drive(jt, rh):
+            bank = next_bank("first", R1)
+            for a in range(2):
+                codes, scales = table_columns(a, jt)
+                nc.tensor.matmul_mx(
+                    out=bank[:],
+                    lhsT=codes,
+                    lhsT_scale=scales,
+                    rhs=w1_codes[:, a, 2 * PASS * rh : 2 * PASS * (rh + 1)].bitcast(E2M1),
+                    rhs_scale=w1_plane[:, a, PASS * rh : PASS * (rh + 1)],
+                    start=(a == 0),
+                    stop=(a == 1),
+                )
+            h_rows[jt, rh] = ring.tile([P, PASS], BF16, name="h_rows", bufs=12)
             nc.vector.tensor_tensor(
                 h_rows[jt, rh][:].rearrange("j (u p e) -> j u p e", u=2, e=2),
-                in_word_order(drive),
-                factor[:].rearrange("j (u p e) -> j u p e", u=2, e=2),
+                in_word_order(bank),
+                factors[jt, rh][:].rearrange("j (u p e) -> j u p e", u=2, e=2),
                 ALU.mult,
             )
 
@@ -204,7 +213,7 @@ def tile_list_cap_voxel_update_kernel(
             c, j0 = chunk_of(jt)
             if j0 == 0:
                 h_grouped[c] = ring.tile([P, 2, CHUNKS[c], 2], F32, name="h_grouped", align_bytes=64, bufs=2)
-            turned = acc_bank()[:].rearrange("p (b u j) -> p b u j", b=2, u=2)
+            turned = next_bank("second", R2)[:].rearrange("p (b u j) -> p b u j", b=2, u=2)
             for rh in range(2):
                 words = h_rows[jt, rh][:].bitcast(F32)
                 for u in range(2):
@@ -238,7 +247,7 @@ def tile_list_cap_voxel_update_kernel(
 
         def first_half(c, n):
             ns = slice(P * n, P * (n + 1))
-            bank = acc_bank()[:, : CHUNKS[c]]
+            bank = next_bank("second", R2)[:, : CHUNKS[c]]
             steps_made[c, n] = ring.tile([P, CHUNKS[c]], F32, name="new", bufs=4)
             for b in range(2):
                 nc.tensor.matmul_mx(
@@ -260,21 +269,26 @@ def tile_list_cap_voxel_update_kernel(
                 nc.sync.dma_start(out[P * n : P * (n + 1), :], volume[n][:])
 
         pick_codes(0, 0)
-        pick_scales()
+        pick_scales(0)
+        pick_scales(1)
         quantize_weight(0)
         pick_codes(1, 0)
         for c in range(1, 4):
             quantize_weight(c)
         units = UNITS
         jobs = [(c, n) for c in range(len(CHUNKS)) for n in range(N // P)]
-        job_at = {JOB0 + JOBSTEP * k: job for k, job in enumerate(jobs)}
+        job_at = {(JOBS[k] if k < len(JOBS) else JOBS[-1] + k): job for k, job in enumerate(jobs)}
+        for unit in units[:L]:
+            damp(*unit)
         last = None
         for step in range(max(job_at) + 2):
             if step < len(units):
                 if step == REST and FIRST < S:
                     pick_codes(0, 1)
                     pick_codes(1, 1)
-                damped_drive(*units[step])
+                if step + L < len(units):
+                    damp(*units[step + L])
+                drive(*units[step])
             if step in W3:
                 quantize_weight(4 + W3.index(step))
             if TL <= step < len(units) + TL and units[step - TL][1] == 1:

@@ -1,7 +1,6 @@
 from contextlib import ExitStack
 
 import concourse.mybir as mybir
-from concourse.masks import make_identity
 
 K, H, N, T, S = 1024, 1024, 512, 2048, 1024
 FLOPS = 2 * S * (2 * K * H + H * N)
@@ -19,25 +18,21 @@ ALU = mybir.AluOpType
 
 P = 128
 PASS = 512
-ON_VECTOR = (0, 0, 0, 512, 512, 0)
-CHUNKS = (256, 256, 512)
-RING = 4
-JOB0 = 10
-JOBSTEP = 2
-W3 = (4, 5)
-PICKS = (4, 5, 6, 7)
-REST = 0
-FIRST = 1024
-LOADS = "t0 s t1 c0 c1 c2 c3 w g0 c4 c5 g1 g2 g3"
-UNITS = [(jt, rh) for c in range(4) for rh in range(2) for jt in (2 * c, 2 * c + 1)]
-TL = 4
-WARM = 1
-L = 2
-R1 = 6
-R2 = 2
-JOBS = (7, 8, 9, 10, 13, 15, 18, 19)
-FB = 8
-PW = 1024
+CHUNK = 256
+ON_VECTOR = (0, 2, 4, 4, 4, 4)
+LOADS = "t0 s c0 t1 x c1 c2 w m c3 c4 c5 g0 g1 g2 g3"
+FUSED = (0, 1, 2, 3)
+ON_GPSIMD = ()
+PREPARE = "0 1 2 w 3"
+HOSTS = {(0, 0): (4, 0), (0, 1): (5, 0)}
+ROOT_BUFS = 3
+SIZE_BUFS = 3
+LEAD = 0
+JOB0 = 4
+W3_STEP = (0, 2)
+SUM_BUFS = 2
+BANKS = (3, 3, 2)
+FACTOR_BUFS = 4
 
 
 def tile_list_cap_voxel_update_kernel(
@@ -52,84 +47,84 @@ def tile_list_cap_voxel_update_kernel(
         offsets = keep.tile([P, S // 16], U16, name="offsets")
         nc.sync.dma_start(offsets[:], offs)
 
-        tab_plane = keep.tile([P, 2, T], U8, name="tab_plane", align_bytes=64)
+        tab_plane = keep.tile([P, T], U8, name="tab_plane", align_bytes=64)
         w1_plane = keep.tile([P, 2, H], U8, name="w1_plane", align_bytes=64)
+        v_moved = keep.tile([P, S], U8, name="v_moved", align_bytes=64)
         nc.gpsimd.memset(tab_plane[:].bitcast(I32), 0)
         nc.vector.memset(w1_plane[:].bitcast(I32), 0)
+        nc.vector.memset(v_moved[:].bitcast(I32), 0)
 
-        tab, raws = {}, {}
+        warm = keep.tile([P, 2], F32, name="warm")
+        nc.vector.memset(warm[:, :1], 1.0)
+        nc.scalar.activation(warm[:, 1:], warm[:, :1], ACT.Abs_reciprocal_sqrt)
 
-        def load_table(a):
-            tab[a] = keep.tile([P, T], U32, name="tab%d" % a)
-            nc.sync.dma_start(
-                tab[a][:].bitcast(I32), tab_words[a].rearrange("p t i -> p (t i)").bitcast(I32)
-            )
+        tab, raws, volume = {}, {}, {}
+        w1_raw = keep.tile([P, 2, 2 * H], U8, name="w1_raw", align_bytes=64)
+        v_scales = keep.tile([P, S], U8, name="v_scales", align_bytes=64)
+        v_codes = {}
 
-        blocks = [w2[PASS * a : PASS * (a + 1), PASS * rh : PASS * (rh + 1)] for rh in range(2) for a in range(2)]
-        blocks = blocks + [w3[PASS * b : PASS * (b + 1), :] for b in range(2)]
+        def pick_codes(a):
+            v_codes[a] = keep.tile([P, S], U32, name="v_codes%d" % a, align_bytes=64)
+            nc.vector.tensor_copy(v_codes[a][:], tab[a][:].indirect(offsets[:]))
 
-        def load_weight(c):
-            raws[c] = keep.tile([P, 4, PASS], F32, name="raw%d" % c)
-            nc.sync.dma_start(raws[c][:], blocks[c].rearrange("(p i) c -> p i c", i=4))
-
-        w1_codes = keep.tile([P, 2, 2 * H], U8, name="w1_codes", align_bytes=64)
-        volume = {}
         for item in LOADS.split():
             if item[0] == "t":
-                load_table(int(item[1]))
+                a = int(item[1])
+                tab[a] = keep.tile([P, T], U32, name="tab%d" % a)
+                nc.sync.dma_start(
+                    tab[a][:].bitcast(I32), tab_words[a].rearrange("p t i -> p (t i)").bitcast(I32)
+                )
+                pick_codes(a)
+            if item == "s":
+                for q in range(4):
+                    nc.sync.dma_start(
+                        tab_plane[32 * q : 32 * q + 8, :].bitcast(I32),
+                        tab_scales[:, 4 * q : 4 * q + 4, :].bitcast(I32),
+                    )
+                nc.vector.tensor_copy(v_scales[:], tab_plane[:].indirect(offsets[:]))
+            if item == "m":
+                nc.sync.dma_start(v_moved[0:112, :].bitcast(I32), v_scales[4:116, :].bitcast(I32))
             if item[0] == "c":
-                load_weight(int(item[1]))
+                c = int(item[1])
+                raws[c] = keep.tile([P, 4, PASS], F32, name="raw%d" % c, align_bytes=64)
+                if c < 4:
+                    b, a = divmod(c, 2)
+                    block = w2[PASS * a : PASS * (a + 1), PASS * b : PASS * (b + 1)]
+                    nc.sync.dma_start(raws[c][:], block.rearrange("(p i) c -> p i c", i=4))
+                else:
+                    b = c - 4
+                    rows = w3[PASS * b : PASS * (b + 1), :].rearrange("(m t e) n -> t m e n", t=4, e=4)
+                    for t in range(4):
+                        nc.sync.dma_start(raws[c][:, t, :], rows[t])
             if item[0] == "g":
                 n = int(item[1])
                 volume[n] = keep.tile([P, T], F32, name="volume%d" % n)
                 nc.sync.dma_start(volume[n][:], gT[P * n : P * (n + 1), :])
-            if item == "s":
-                for q in range(4):
-                    nc.sync.dma_start(
-                        tab_plane[32 * q : 32 * q + 4, :, :].bitcast(I32),
-                        tab_scales[:, 4 * q : 4 * q + 4, :].rearrange("a r t -> r a t").bitcast(I32),
-                    )
             if item == "w":
                 nc.sync.dma_start(
-                    w1_codes[:].bitcast(I32), w1_words.rearrange("a p c -> p a c").bitcast(I32)
+                    w1_raw[:].bitcast(I32), w1_words.rearrange("a p c -> p a c").bitcast(I32)
                 )
+            if item == "x":
                 for q in range(4):
                     nc.sync.dma_start(
                         w1_plane[32 * q : 32 * q + 4, :, :].bitcast(I32),
                         w1_scales[:, 4 * q : 4 * q + 4, :].rearrange("a r c -> r a c").bitcast(I32),
                     )
 
-        if WARM:
-            warm = keep.tile([P, 2], F32, name="warm")
-            nc.vector.memset(warm[:, :1], 1.0)
-            nc.scalar.activation(warm[:, 1:], warm[:, :1], ACT.Abs_reciprocal_sqrt)
-
-        ident = keep.tile([P, P], F32, name="ident")
-        make_identity(nc, ident[:])
-
-        v_codes = {}
-
-        def pick_codes(a, part):
-            j0, j1 = ((0, FIRST), (FIRST, S))[part]
-            v_codes[a, part] = keep.tile([P, j1 - j0], U32, name="v_codes%d%d" % (a, part), align_bytes=64)
-            nc.vector.tensor_copy(v_codes[a, part][:], tab[a][:].indirect(offsets[:, j0 // 16 : j1 // 16]))
-
-        v_scales = {}
-
-        def pick_scales(a):
-            v_scales[a] = keep.tile([P, S], U8, name="v_scales%d" % a, align_bytes=64)
-            nc.vector.tensor_copy(v_scales[a][:], tab_plane[:, a, :].indirect(offsets[:]))
-
         w_codes, w_scales = {}, {}
 
         def quantize_weight(c):
             grouped = ring.tile([P, PASS, 4], BF16, name="grouped", align_bytes=64)
-            dst = grouped[:].rearrange("p (c k) i -> p c i k", k=4)
-            src = raws[c][:].rearrange("p i (c k) -> p c i k", k=4)
-            cut = ON_VECTOR[c] // 4
+            cut = ON_VECTOR[c]
+            if c < 4:
+                dst = grouped[:].rearrange("p (t m e) i -> p t m i e", t=4, e=4)
+                src = raws[c][:].rearrange("p i (m t e) -> p t m i e", t=4, e=4)
+            else:
+                dst = grouped[:].rearrange("p (t m e) i -> p t m i e", t=4, e=4)
+                src = raws[c][:].rearrange("p i (t m e) -> p t m i e", t=4, e=4)
             if cut > 0:
                 nc.vector.tensor_copy(dst[:, :cut], src[:, :cut])
-            if cut < PASS // 4:
+            if cut < 4:
                 nc.scalar.copy(dst[:, cut:], src[:, cut:])
             w_codes[c] = keep.tile([P, PASS], U32, name="w_codes%d" % c, align_bytes=64)
             w_scales[c] = keep.tile([P, PASS], U8, name="w_scales%d" % c, align_bytes=64)
@@ -139,7 +134,20 @@ def tile_list_cap_voxel_update_kernel(
                 in_=grouped[:].rearrange("p c i -> p (c i)"),
             )
 
-        taken = {"first": 0, "second": 0}
+        w1_codes = keep.tile([P, 4 * H], U8, name="w1_codes", align_bytes=64)
+        w1_dealt = keep.tile([P, 2 * H], U8, name="w1_dealt", align_bytes=64)
+
+        def deal_w1():
+            nc.vector.tensor_copy(
+                w1_codes[:].bitcast(I32).rearrange("p (g t m w) -> p g t m w", g=4, t=4, w=2),
+                w1_raw[:].bitcast(I32).rearrange("p a (b m t w) -> p (a b) t m w", b=2, t=4, w=2),
+            )
+            nc.vector.tensor_copy(
+                w1_dealt[:].bitcast(I32).rearrange("p (g t m) -> p g t m", g=4, t=4),
+                w1_plane[:].bitcast(I32).rearrange("p a (b m t) -> p (a b) t m", b=2, t=4),
+            )
+
+        taken = {"damping": 0, "drive": 0, "change": 0}
 
         def next_bank(stage, depth):
             bank = psum.tile([P, PASS], F32, name="%s%d" % (stage, taken[stage] % depth))
@@ -147,160 +155,143 @@ def tile_list_cap_voxel_update_kernel(
             return bank
 
         def in_word_order(bank):
-            return bank[:].rearrange("j (p u e) -> j u p e", u=2, e=2)
+            return bank[:].rearrange("p (t j) -> p j t", t=4)
 
-        h_rows = {}
+        def as_words(tile):
+            return tile.rearrange("p (j t) -> p j t", t=4)
 
-        factors = {}
+        sizes, roots, factors = {}, {}, {}
 
-        def table_columns(a, jt):
-            part = min(P * jt // FIRST, 1)
-            codes = v_codes[a, part][:, P * jt - FIRST * part : P * (jt + 1) - FIRST * part]
-            return codes.bitcast(E4M3), v_scales[a][:, P * jt : P * (jt + 1)]
+        def damp(u):
+            jt, b = units[u]
+            js = slice(P * jt, P * (jt + 1))
+            bank = next_bank("damping", BANKS[0])
+            for t in range(4):
+                ts = slice(P * t, P * (t + 1))
+                for a in range(2):
+                    nc.tensor.matmul_mx(
+                        out=bank[:, ts],
+                        lhsT=w_codes[2 * b + a][:, ts].bitcast(E4M3),
+                        lhsT_scale=w_scales[2 * b + a][:, ts],
+                        rhs=v_codes[a][:, js].bitcast(E4M3),
+                        rhs_scale=v_scales[4 * a :, js],
+                        start=(a == 0),
+                        stop=(a == 1),
+                    )
+            sizes[u] = ring.tile([P, PASS], F32, name="size", bufs=SIZE_BUFS)
+            nc.scalar.activation(as_words(sizes[u][:]), in_word_order(bank), ACT.Abs)
 
-        def damp(jt, rh):
-            damping = next_bank("first", R1)
-            for a in range(2):
-                codes, scales = table_columns(a, jt)
-                nc.tensor.matmul_mx(
-                    out=damping[:],
-                    lhsT=codes,
-                    lhsT_scale=scales,
-                    rhs=w_codes[2 * rh + a][:].bitcast(E4M3),
-                    rhs_scale=w_scales[2 * rh + a][:],
-                    start=(a == 0),
-                    stop=(a == 1),
-                )
-            size = ring.tile([P, PASS], F32, name="size")
-            nc.scalar.activation(
-                size[:].rearrange("j (u p e) -> j u p e", u=2, e=2), in_word_order(damping), ACT.Abs
-            )
-            root = ring.tile([P, PASS], F32, name="root")
-            nc.scalar.activation(root[:], size[:], ACT.Abs_reciprocal_sqrt, bias=1.0)
-            factors[jt, rh] = ring.tile([P, PASS], F32, name="factor", bufs=FB)
-            nc.scalar.activation(factors[jt, rh][:], root[:], ACT.Square)
+        def root(u):
+            roots[u] = ring.tile([P, PASS], F32, name="root", bufs=ROOT_BUFS)
+            nc.scalar.activation(roots[u][:], sizes[u][:], ACT.Abs_reciprocal_sqrt, bias=1.0)
 
-        def drive(jt, rh):
-            bank = next_bank("first", R1)
-            for a in range(2):
-                codes, scales = table_columns(a, jt)
-                nc.tensor.matmul_mx(
-                    out=bank[:],
-                    lhsT=codes,
-                    lhsT_scale=scales,
-                    rhs=w1_codes[:, a, 2 * PASS * rh : 2 * PASS * (rh + 1)].bitcast(E2M1),
-                    rhs_scale=w1_plane[:, a, PASS * rh : PASS * (rh + 1)],
-                    start=(a == 0),
-                    stop=(a == 1),
-                )
-            h_rows[jt, rh] = ring.tile([P, PASS], BF16, name="h_rows", bufs=12)
-            nc.vector.tensor_tensor(
-                h_rows[jt, rh][:].rearrange("j (u p e) -> j u p e", u=2, e=2),
-                in_word_order(bank),
-                factors[jt, rh][:].rearrange("j (u p e) -> j u p e", u=2, e=2),
-                ALU.mult,
-            )
-
-        starts = [sum(CHUNKS[:c]) for c in range(len(CHUNKS) + 1)]
-
-        def chunk_of(jt):
-            c = max(k for k in range(len(CHUNKS)) if starts[k] <= P * jt)
-            return c, P * jt - starts[c]
+        def square(u):
+            if u in ON_GPSIMD:
+                factors[u] = roots[u]
+            else:
+                factors[u] = ring.tile([P, PASS], F32, name="factor", bufs=FACTOR_BUFS)
+                nc.scalar.activation(factors[u][:], roots[u][:], ACT.Square)
 
         h_grouped = {}
 
-        def turn(jt):
-            c, j0 = chunk_of(jt)
-            if j0 == 0:
-                h_grouped[c] = ring.tile([P, 2, CHUNKS[c], 2], F32, name="h_grouped", align_bytes=64, bufs=2)
-            turned = next_bank("second", R2)[:].rearrange("p (b u j) -> p b u j", b=2, u=2)
-            for rh in range(2):
-                words = h_rows[jt, rh][:].bitcast(F32)
-                for u in range(2):
-                    nc.tensor.transpose(turned[:, rh, u, :], words[:, P * u : P * (u + 1)], ident[:])
-            nc.scalar.copy(
-                h_grouped[c][:, :, j0 : j0 + P, :], turned.rearrange("p b u j -> p b j u")
-            )
+        def drive(u):
+            jt, b = units[u]
+            js = slice(P * jt, P * (jt + 1))
+            c, j0 = divmod(P * jt, CHUNK)
+            if (c, b) not in h_grouped:
+                if (c, b) in HOSTS:
+                    host = raws[HOSTS[c, b][0]][:].rearrange("p i c -> p (i c)").bitcast(BF16)
+                    h_grouped[c, b] = host[:, 4 * CHUNK * HOSTS[c, b][1] : 4 * CHUNK * (HOSTS[c, b][1] + 1)]
+                else:
+                    h_grouped[c, b] = ring.tile([P, 4 * CHUNK], BF16, name="h_grouped", align_bytes=64, bufs=3)[:]
+            bank = next_bank("drive", BANKS[1])
+            for t in range(4):
+                for a in range(2):
+                    col = P * ((2 * a + b) * 4 + t)
+                    nc.tensor.matmul_mx(
+                        out=bank[:, P * t : P * (t + 1)],
+                        lhsT=w1_codes[:, 2 * col : 2 * (col + P)].bitcast(E2M1),
+                        lhsT_scale=w1_dealt[:, col : col + P],
+                        rhs=v_codes[a][:, js].bitcast(E4M3),
+                        rhs_scale=(v_scales, v_moved)[a][:, js],
+                        start=(a == 0),
+                        stop=(a == 1),
+                    )
+            h_part = h_grouped[c, b][:, 4 * j0 : 4 * (j0 + P)]
+            if u in ON_GPSIMD:
+                plain = ring.tile([P, PASS], F32, name="plain", bufs=2)
+                nc.scalar.copy(as_words(plain[:]), in_word_order(bank))
+                half = ring.tile([P, PASS], F32, name="half", bufs=2)
+                nc.gpsimd.tensor_tensor(half[:], plain[:], factors[u][:], ALU.mult)
+                nc.gpsimd.tensor_tensor(h_part, half[:], factors[u][:], ALU.mult)
+            else:
+                nc.vector.tensor_tensor(as_words(h_part), in_word_order(bank), as_words(factors[u][:]), ALU.mult)
 
         h_codes, h_scales = {}, {}
 
-        def quantize_h(c):
-            h_codes[c] = keep.tile([P, 2, CHUNKS[c]], U32, name="h_codes%d" % c, align_bytes=64)
-            h_scales[c] = keep.tile([P, 2, CHUNKS[c]], U8, name="h_scales%d" % c, align_bytes=64)
+        def quantize_h(c, b):
+            h_codes[c, b] = keep.tile([P, CHUNK], U32, name="h_codes%d%d" % (c, b), align_bytes=64)
+            h_scales[c, b] = keep.tile([P, CHUNK], U8, name="h_scales%d%d" % (c, b), align_bytes=64)
             nc.vector.quantize_mx(
-                out=h_codes[c][:].rearrange("p b j -> p (b j)").bitcast(E4M3),
-                scales=h_scales[c][:].rearrange("p b j -> p (b j)"),
-                in_=h_grouped[c][:].rearrange("p b j u -> p (b j u)").bitcast(BF16),
+                out=h_codes[c, b][:].bitcast(E4M3), scales=h_scales[c, b][:], in_=h_grouped[c, b]
             )
 
         def listed(c, n):
-            return volume[n][:].indirect(offsets[:, starts[c] // 16 : starts[c + 1] // 16])
+            return volume[n][:].indirect(offsets[:, CHUNK * c // 16 : CHUNK * (c + 1) // 16])
 
-        picked = {}
-
-        def pick_old(n):
-            picked[n] = keep.tile([P, S], F32, name="picked%d" % n)
-            for j0 in range(0, S, PW):
-                nc.vector.tensor_copy(picked[n][:, j0 : j0 + PW], volume[n][:].indirect(offsets[:, j0 // 16 : (j0 + PW) // 16]))
-
-        steps_made = {}
+        picked, totals = {}, {}
 
         def first_half(c, n):
             ns = slice(P * n, P * (n + 1))
-            bank = next_bank("second", R2)[:, : CHUNKS[c]]
-            steps_made[c, n] = ring.tile([P, CHUNKS[c]], F32, name="new", bufs=4)
+            if c == 0 and n not in FUSED:
+                picked[n] = keep.tile([P, S], F32, name="picked%d" % n)
+                nc.vector.tensor_copy(picked[n][:], volume[n][:].indirect(offsets[:]))
+            bank = next_bank("change", BANKS[2])[:, :CHUNK]
             for b in range(2):
                 nc.tensor.matmul_mx(
                     out=bank,
                     lhsT=w_codes[4 + b][:, ns].bitcast(E4M3),
                     lhsT_scale=w_scales[4 + b][:, ns],
-                    rhs=h_codes[c][:, b, :].bitcast(E4M3),
-                    rhs_scale=h_scales[c][:, b, :],
+                    rhs=h_codes[c, b][:].bitcast(E4M3),
+                    rhs_scale=h_scales[c, b][:],
                     start=(b == 0),
                     stop=(b == 1),
                 )
-            old = picked[n][:, starts[c] : starts[c + 1]]
-            nc.vector.scalar_tensor_tensor(steps_made[c, n][:], old, -1.0, bank, op0=ALU.mult, op1=ALU.max)
+            total = ring.tile([P, CHUNK], F32, name="total", bufs=SUM_BUFS)
+            if n in FUSED:
+                change = ring.tile([P, CHUNK], F32, name="change", bufs=2)
+                nc.scalar.copy(change[:], bank)
+                nc.vector.tensor_tensor(total[:], listed(c, n), change[:], ALU.add)
+            else:
+                nc.vector.tensor_tensor(total[:], bank, picked[n][:, CHUNK * c : CHUNK * (c + 1)], ALU.add)
+            totals[c, n] = total
 
         def second_half(c, n):
-            old = picked[n][:, starts[c] : starts[c + 1]]
-            nc.vector.tensor_tensor(listed(c, n), old, steps_made[c, n][:], ALU.add)
-            if c == len(CHUNKS) - 1:
+            new = ring.tile([P, CHUNK], F32, name="new", bufs=2)
+            nc.scalar.activation(new[:], totals[c, n][:], ACT.Relu)
+            nc.vector.tensor_copy(listed(c, n), new[:])
+            if c == S // CHUNK - 1:
                 nc.sync.dma_start(out[P * n : P * (n + 1), :], volume[n][:])
 
-        pick_codes(0, 0)
-        pick_scales(0)
-        pick_scales(1)
-        quantize_weight(0)
-        pick_codes(1, 0)
-        for c in range(1, 4):
-            quantize_weight(c)
-        units = UNITS
-        jobs = [(c, n) for c in range(len(CHUNKS)) for n in range(N // P)]
-        job_at = {(JOBS[k] if k < len(JOBS) else JOBS[-1] + k): job for k, job in enumerate(jobs)}
-        for unit in units[:L]:
-            damp(*unit)
-        last = None
-        for step in range(max(job_at) + 2):
-            if step < len(units):
-                if step == REST and FIRST < S:
-                    pick_codes(0, 1)
-                    pick_codes(1, 1)
-                if step + L < len(units):
-                    damp(*units[step + L])
-                drive(*units[step])
-            if step in W3:
-                quantize_weight(4 + W3.index(step))
-            if TL <= step < len(units) + TL and units[step - TL][1] == 1:
-                jt = units[step - TL][0]
-                turn(jt)
-                c, j0 = chunk_of(jt)
-                if j0 + P == CHUNKS[c]:
-                    quantize_h(c)
-            if step in PICKS:
-                pick_old(PICKS.index(step))
-            if step in job_at:
-                first_half(*job_at[step])
-            if last:
-                second_half(*last)
-            last = job_at.get(step)
+        units = [(jt, b) for c in range(S // CHUNK) for b in range(2) for jt in (2 * c, 2 * c + 1)]
+        jobs = [(c, n) for c in range(S // CHUNK) for n in range(N // P)]
+        for item in PREPARE.split():
+            if item == "w":
+                deal_w1()
+            else:
+                quantize_weight(int(item))
+        for step in range(-2 - LEAD, JOB0 + len(jobs) + 1):
+            for ahead, stage in ((2, damp), (1, root), (0, square)):
+                if 0 <= step + LEAD + ahead < len(units):
+                    stage(step + LEAD + ahead)
+            if step in W3_STEP:
+                quantize_weight(4 + W3_STEP.index(step))
+            if 0 <= step < len(units):
+                drive(step)
+                jt, b = units[step]
+                if jt % 2 == 1:
+                    quantize_h(jt // 2, b)
+            if 0 <= step - JOB0 < len(jobs):
+                first_half(*jobs[step - JOB0])
+            if 0 <= step - JOB0 - 1 < len(jobs):
+                second_half(*jobs[step - JOB0 - 1])

@@ -20,15 +20,15 @@ P = 128
 PASS = 512
 CHUNK = 256
 ON_VECTOR = (0, 2, 4, 4, 4, 4)
-LOADS = "t0 s c0 t1 x c1 c2 w m c3 c4 c5 g0 g1 g2 g3"
-FUSED = (0, 1, 2, 3)
-ON_GPSIMD = ()
+LOADS = "t0 s t1 c0 c1 x c2 w m c3 c4 c5 g0 g1 g2 g3"
+FUSED = (1,2,3)
+ON_GPSIMD = (6,8,10,12,14)
 PREPARE = "0 1 2 w 3"
 HOSTS = {(0, 0): (4, 0), (0, 1): (5, 0)}
 ROOT_BUFS = 3
 SIZE_BUFS = 3
+JOB_STEPS = tuple(range(5, 20))
 LEAD = 0
-JOB0 = 4
 W3_STEP = (0, 2)
 SUM_BUFS = 2
 BANKS = (3, 3, 2)
@@ -54,9 +54,10 @@ def tile_list_cap_voxel_update_kernel(
         nc.vector.memset(w1_plane[:].bitcast(I32), 0)
         nc.vector.memset(v_moved[:].bitcast(I32), 0)
 
-        warm = keep.tile([P, 2], F32, name="warm")
-        nc.vector.memset(warm[:, :1], 1.0)
-        nc.scalar.activation(warm[:, 1:], warm[:, :1], ACT.Abs_reciprocal_sqrt)
+        ones = keep.tile([P, 3], F32, name="ones")
+        nc.vector.memset(ones[:, 0:1], 1.0)
+        nc.scalar.activation(ones[:, 1:2], ones[:, 0:1], ACT.Abs_reciprocal_sqrt)
+        nc.scalar.activation(ones[:, 2:3], ones[:, 1:2], ACT.Sign)
 
         tab, raws, volume = {}, {}, {}
         w1_raw = keep.tile([P, 2, 2 * H], U8, name="w1_raw", align_bytes=64)
@@ -168,31 +169,28 @@ def tile_list_cap_voxel_update_kernel(
             bank = next_bank("damping", BANKS[0])
             for t in range(4):
                 ts = slice(P * t, P * (t + 1))
-                for a in range(2):
+                for a in (1, 0):
                     nc.tensor.matmul_mx(
                         out=bank[:, ts],
                         lhsT=w_codes[2 * b + a][:, ts].bitcast(E4M3),
                         lhsT_scale=w_scales[2 * b + a][:, ts],
                         rhs=v_codes[a][:, js].bitcast(E4M3),
                         rhs_scale=v_scales[4 * a :, js],
-                        start=(a == 0),
-                        stop=(a == 1),
+                        start=(a == 1),
+                        stop=(a == 0),
                     )
             sizes[u] = ring.tile([P, PASS], F32, name="size", bufs=SIZE_BUFS)
             nc.scalar.activation(as_words(sizes[u][:]), in_word_order(bank), ACT.Abs)
 
         def root(u):
             roots[u] = ring.tile([P, PASS], F32, name="root", bufs=ROOT_BUFS)
-            nc.scalar.activation(roots[u][:], sizes[u][:], ACT.Abs_reciprocal_sqrt, bias=1.0)
+            nc.scalar.activation(roots[u][:], sizes[u][:], ACT.Abs_reciprocal_sqrt, bias=ones[:, 2:3])
 
         def square(u):
-            if u in ON_GPSIMD:
-                factors[u] = roots[u]
-            else:
-                factors[u] = ring.tile([P, PASS], F32, name="factor", bufs=FACTOR_BUFS)
-                nc.scalar.activation(factors[u][:], roots[u][:], ACT.Square)
+            factors[u] = ring.tile([P, PASS], F32, name="factor", bufs=FACTOR_BUFS)
+            nc.scalar.activation(factors[u][:], roots[u][:], ACT.Square)
 
-        h_grouped = {}
+        h_grouped, h_parts, plains = {}, {}, {}
 
         def drive(u):
             jt, b = units[u]
@@ -218,12 +216,10 @@ def tile_list_cap_voxel_update_kernel(
                         stop=(a == 1),
                     )
             h_part = h_grouped[c, b][:, 4 * j0 : 4 * (j0 + P)]
+            h_parts[u] = h_part
             if u in ON_GPSIMD:
-                plain = ring.tile([P, PASS], F32, name="plain", bufs=2)
-                nc.scalar.copy(as_words(plain[:]), in_word_order(bank))
-                half = ring.tile([P, PASS], F32, name="half", bufs=2)
-                nc.gpsimd.tensor_tensor(half[:], plain[:], factors[u][:], ALU.mult)
-                nc.gpsimd.tensor_tensor(h_part, half[:], factors[u][:], ALU.mult)
+                plains[u] = ring.tile([P, PASS], F32, name="plain", bufs=2)
+                nc.scalar.copy(as_words(plains[u][:]), in_word_order(bank))
             else:
                 nc.vector.tensor_tensor(as_words(h_part), in_word_order(bank), as_words(factors[u][:]), ALU.mult)
 
@@ -236,51 +232,60 @@ def tile_list_cap_voxel_update_kernel(
                 out=h_codes[c, b][:].bitcast(E4M3), scales=h_scales[c, b][:], in_=h_grouped[c, b]
             )
 
-        def listed(c, n):
-            return volume[n][:].indirect(offsets[:, CHUNK * c // 16 : CHUNK * (c + 1) // 16])
+        def listed(c0, c1, n):
+            return volume[n][:].indirect(offsets[:, CHUNK * c0 // 16 : CHUNK * c1 // 16])
 
         picked, totals = {}, {}
 
-        def first_half(c, n):
+        def first_half(c0, c1, n, step):
             ns = slice(P * n, P * (n + 1))
-            if c == 0 and n not in FUSED:
+            width = CHUNK * (c1 - c0)
+            if c0 == 0 and n not in FUSED:
                 picked[n] = keep.tile([P, S], F32, name="picked%d" % n)
                 nc.vector.tensor_copy(picked[n][:], volume[n][:].indirect(offsets[:]))
-            bank = next_bank("change", BANKS[2])[:, :CHUNK]
-            for b in range(2):
-                nc.tensor.matmul_mx(
-                    out=bank,
-                    lhsT=w_codes[4 + b][:, ns].bitcast(E4M3),
-                    lhsT_scale=w_scales[4 + b][:, ns],
-                    rhs=h_codes[c, b][:].bitcast(E4M3),
-                    rhs_scale=h_scales[c, b][:],
-                    start=(b == 0),
-                    stop=(b == 1),
-                )
-            total = ring.tile([P, CHUNK], F32, name="total", bufs=SUM_BUFS)
-            if n in FUSED:
-                change = ring.tile([P, CHUNK], F32, name="change", bufs=2)
-                nc.scalar.copy(change[:], bank)
-                nc.vector.tensor_tensor(total[:], listed(c, n), change[:], ALU.add)
+            bank = next_bank("change", BANKS[2])[:, :width]
+            for c in range(c0, c1):
+                for b in (1, 0):
+                    nc.tensor.matmul_mx(
+                        out=bank[:, CHUNK * (c - c0) : CHUNK * (c - c0 + 1)],
+                        lhsT=w_codes[4 + b][:, ns].bitcast(E4M3),
+                        lhsT_scale=w_scales[4 + b][:, ns],
+                        rhs=h_codes[c, b][:].bitcast(E4M3),
+                        rhs_scale=h_scales[c, b][:],
+                        start=(b == 1),
+                        stop=(b == 0),
+                    )
+            total = ring.tile([P, width], F32, name="total", bufs=SUM_BUFS)
+            if n not in FUSED:
+                nc.vector.tensor_tensor(total[:], bank, picked[n][:, CHUNK * c0 : CHUNK * c1], ALU.add)
             else:
-                nc.vector.tensor_tensor(total[:], bank, picked[n][:, CHUNK * c : CHUNK * (c + 1)], ALU.add)
-            totals[c, n] = total
+                if step in ON_GPSIMD:
+                    change = h_parts[step].bitcast(F32)
+                else:
+                    change = ring.tile([P, width], F32, name="change", bufs=2)[:]
+                nc.scalar.copy(change, bank)
+                nc.vector.tensor_tensor(total[:], listed(c0, c1, n), change, ALU.add)
+            totals[c0, n] = total
 
-        def second_half(c, n):
-            new = ring.tile([P, CHUNK], F32, name="new", bufs=2)
-            nc.scalar.activation(new[:], totals[c, n][:], ACT.Relu)
-            nc.vector.tensor_copy(listed(c, n), new[:])
-            if c == S // CHUNK - 1:
+        def second_half(c0, c1, n, step):
+            width = CHUNK * (c1 - c0)
+            if step == len(units) - 1:
+                new = factors[step][:, :width]
+            else:
+                new = ring.tile([P, width], F32, name="new", bufs=2)[:]
+            nc.scalar.activation(new, totals[c0, n][:], ACT.Relu)
+            nc.vector.tensor_copy(listed(c0, c1, n), new)
+            if c1 == S // CHUNK:
                 nc.sync.dma_start(out[P * n : P * (n + 1), :], volume[n][:])
 
         units = [(jt, b) for c in range(S // CHUNK) for b in range(2) for jt in (2 * c, 2 * c + 1)]
-        jobs = [(c, n) for c in range(S // CHUNK) for n in range(N // P)]
+        jobs = [(c, c + 1, n) for c in range(4) for n in range(4) if c < 2 or n < 3] + [(2, 4, 3)]
         for item in PREPARE.split():
             if item == "w":
                 deal_w1()
             else:
                 quantize_weight(int(item))
-        for step in range(-2 - LEAD, JOB0 + len(jobs) + 1):
+        for step in range(-2 - LEAD, JOB_STEPS[-1] + 2):
             for ahead, stage in ((2, damp), (1, root), (0, square)):
                 if 0 <= step + LEAD + ahead < len(units):
                     stage(step + LEAD + ahead)
@@ -288,10 +293,11 @@ def tile_list_cap_voxel_update_kernel(
                 quantize_weight(4 + W3_STEP.index(step))
             if 0 <= step < len(units):
                 drive(step)
-                jt, b = units[step]
-                if jt % 2 == 1:
-                    quantize_h(jt // 2, b)
-            if 0 <= step - JOB0 < len(jobs):
-                first_half(*jobs[step - JOB0])
-            if 0 <= step - JOB0 - 1 < len(jobs):
-                second_half(*jobs[step - JOB0 - 1])
+            if step in JOB_STEPS:
+                first_half(*jobs[JOB_STEPS.index(step)], step)
+            if step in ON_GPSIMD:
+                nc.gpsimd.tensor_tensor(h_parts[step], plains[step][:], factors[step][:], ALU.mult)
+            if 0 <= step < len(units) and units[step][0] % 2 == 1:
+                quantize_h(units[step][0] // 2, units[step][1])
+            if step - 1 in JOB_STEPS:
+                second_half(*jobs[JOB_STEPS.index(step - 1)], step)

@@ -22,12 +22,13 @@ CHUNK = 256
 ON_VECTOR = (0, 2, 4, 4, 4, 4)
 LOADS = "t0 s t1 c0 c1 x c2 w m c3 c4 c5 g0 g1 g2 g3"
 FUSED = (1,2,3)
-ON_GPSIMD = (6,8,10,12,14)
+ON_GPSIMD = (6,8,10,12,13,14)
 PREPARE = "0 1 2 w 3"
 HOSTS = {(0, 0): (4, 0), (0, 1): (5, 0)}
 ROOT_BUFS = 3
 SIZE_BUFS = 3
 JOB_STEPS = tuple(range(5, 20))
+TWICE = ()
 LEAD = 0
 W3_STEP = (0, 2)
 SUM_BUFS = 2
@@ -123,17 +124,21 @@ def tile_list_cap_voxel_update_kernel(
             else:
                 dst = grouped[:].rearrange("p (t m e) i -> p t m i e", t=4, e=4)
                 src = raws[c][:].rearrange("p i (t m e) -> p t m i e", t=4, e=4)
-            if cut > 0:
-                nc.vector.tensor_copy(dst[:, :cut], src[:, :cut])
-            if cut < 4:
-                nc.scalar.copy(dst[:, cut:], src[:, cut:])
             w_codes[c] = keep.tile([P, PASS], U32, name="w_codes%d" % c, align_bytes=64)
             w_scales[c] = keep.tile([P, PASS], U8, name="w_scales%d" % c, align_bytes=64)
-            nc.vector.quantize_mx(
-                out=w_codes[c][:].bitcast(E4M3),
-                scales=w_scales[c][:],
-                in_=grouped[:].rearrange("p c i -> p (c i)"),
-            )
+            for half in range(2):
+                ts = slice(2 * half, 2 * half + 2)
+                if 2 * half < cut:
+                    nc.vector.tensor_copy(dst[:, ts], src[:, ts])
+                else:
+                    nc.scalar.copy(dst[:, ts], src[:, ts])
+            for half in range(2):
+                cols = slice(2 * P * half, 2 * P * (half + 1))
+                nc.vector.quantize_mx(
+                    out=w_codes[c][:, cols].bitcast(E4M3),
+                    scales=w_scales[c][:, cols],
+                    in_=grouped[:, cols, :].rearrange("p c i -> p (c i)"),
+                )
 
         w1_codes = keep.tile([P, 4 * H], U8, name="w1_codes", align_bytes=64)
         w1_dealt = keep.tile([P, 2 * H], U8, name="w1_dealt", align_bytes=64)
@@ -188,7 +193,8 @@ def tile_list_cap_voxel_update_kernel(
 
         def square(u):
             factors[u] = ring.tile([P, PASS], F32, name="factor", bufs=FACTOR_BUFS)
-            nc.scalar.activation(factors[u][:], roots[u][:], ACT.Square)
+            if u not in TWICE:
+                nc.scalar.activation(factors[u][:], roots[u][:], ACT.Square)
 
         h_grouped, h_parts, plains = {}, {}, {}
 
@@ -217,7 +223,7 @@ def tile_list_cap_voxel_update_kernel(
                     )
             h_part = h_grouped[c, b][:, 4 * j0 : 4 * (j0 + P)]
             h_parts[u] = h_part
-            if u in ON_GPSIMD:
+            if u in ON_GPSIMD or u in TWICE:
                 plains[u] = ring.tile([P, PASS], F32, name="plain", bufs=2)
                 nc.scalar.copy(as_words(plains[u][:]), in_word_order(bank))
             else:
@@ -240,9 +246,6 @@ def tile_list_cap_voxel_update_kernel(
         def first_half(c0, c1, n, step):
             ns = slice(P * n, P * (n + 1))
             width = CHUNK * (c1 - c0)
-            if c0 == 0 and n not in FUSED:
-                picked[n] = keep.tile([P, S], F32, name="picked%d" % n)
-                nc.vector.tensor_copy(picked[n][:], volume[n][:].indirect(offsets[:]))
             bank = next_bank("change", BANKS[2])[:, :width]
             for c in range(c0, c1):
                 for b in (1, 0):
@@ -261,6 +264,10 @@ def tile_list_cap_voxel_update_kernel(
             else:
                 if step in ON_GPSIMD:
                     change = h_parts[step].bitcast(F32)
+                elif step in TWICE:
+                    change = factors[step][:, :CHUNK]
+                elif step - 1 in TWICE:
+                    change = h_parts[step - 1].bitcast(F32)
                 else:
                     change = ring.tile([P, width], F32, name="change", bufs=2)[:]
                 nc.scalar.copy(change, bank)
@@ -293,10 +300,17 @@ def tile_list_cap_voxel_update_kernel(
                 quantize_weight(4 + W3_STEP.index(step))
             if 0 <= step < len(units):
                 drive(step)
+            if step == 3:
+                picked[0] = keep.tile([P, S], F32, name="picked")
+                nc.vector.tensor_copy(picked[0][:], volume[0][:].indirect(offsets[:]))
             if step in JOB_STEPS:
                 first_half(*jobs[JOB_STEPS.index(step)], step)
             if step in ON_GPSIMD:
                 nc.gpsimd.tensor_tensor(h_parts[step], plains[step][:], factors[step][:], ALU.mult)
+            if step in TWICE:
+                nc.gpsimd.tensor_tensor(factors[step][:], plains[step][:], roots[step][:], ALU.mult)
+            if step - 1 in TWICE:
+                nc.gpsimd.tensor_tensor(h_parts[step - 1], factors[step - 1][:], roots[step - 1][:], ALU.mult)
             if 0 <= step < len(units) and units[step][0] % 2 == 1:
                 quantize_h(units[step][0] // 2, units[step][1])
             if step - 1 in JOB_STEPS:

@@ -19,21 +19,16 @@ ALU = mybir.AluOpType
 P = 128
 PASS = 512
 CHUNK = 256
-ON_VECTOR = (0, 2, 4, 4, 4, 4)
-LOADS = "t0 s t1 c0 c1 x c2 w m c3 c4 c5 g0 g1 g2 g3"
-FUSED = (1,2,3)
-ON_GPSIMD = (6,8,10,12,13,14)
-PREPARE = "0 1 2 w 3"
-HOSTS = {(0, 0): (4, 0), (0, 1): (5, 0)}
-ROOT_BUFS = 3
-SIZE_BUFS = 3
-JOB_STEPS = tuple(range(5, 20))
-TWICE = ()
-LEAD = 0
-W3_STEP = (0, 2)
-SUM_BUFS = 2
-BANKS = (3, 3, 2)
-FACTOR_BUFS = 4
+CHUNKS = S // CHUNK
+ROW_TILES = N // P
+UNITS = 4 * CHUNKS
+LAST_UNIT = UNITS - 1
+FIRST_UPDATE = 5
+BANKS = {"damping": 3, "drive": 3, "change": 2}
+
+
+def on_gpsimd(u):
+    return FIRST_UPDATE < u < LAST_UNIT and (u % 2 == 0 or u == LAST_UNIT - 2)
 
 
 def tile_list_cap_voxel_update_kernel(
@@ -59,84 +54,75 @@ def tile_list_cap_voxel_update_kernel(
         nc.vector.memset(ones[:, 0:1], 1.0)
         nc.scalar.activation(ones[:, 1:2], ones[:, 0:1], ACT.Abs_reciprocal_sqrt)
         nc.scalar.activation(ones[:, 2:3], ones[:, 1:2], ACT.Sign)
+        one = ones[:, 2:3]
 
-        tab, raws, volume = {}, {}, {}
         w1_raw = keep.tile([P, 2, 2 * H], U8, name="w1_raw", align_bytes=64)
         v_scales = keep.tile([P, S], U8, name="v_scales", align_bytes=64)
-        v_codes = {}
+        v_codes, raws, volume = {}, {}, {}
 
-        def pick_codes(a):
+        def gather_table(a):
+            words = keep.tile([P, T], U32, name="tab%d" % a)
+            nc.sync.dma_start(
+                words[:].bitcast(I32), tab_words[a].rearrange("p t i -> p (t i)").bitcast(I32)
+            )
             v_codes[a] = keep.tile([P, S], U32, name="v_codes%d" % a, align_bytes=64)
-            nc.vector.tensor_copy(v_codes[a][:], tab[a][:].indirect(offsets[:]))
+            nc.vector.tensor_copy(v_codes[a][:], words[:].indirect(offsets[:]))
 
-        for item in LOADS.split():
-            if item[0] == "t":
-                a = int(item[1])
-                tab[a] = keep.tile([P, T], U32, name="tab%d" % a)
+        def gather_table_scales():
+            for q in range(4):
                 nc.sync.dma_start(
-                    tab[a][:].bitcast(I32), tab_words[a].rearrange("p t i -> p (t i)").bitcast(I32)
+                    tab_plane[32 * q : 32 * q + 8, :].bitcast(I32),
+                    tab_scales[:, 4 * q : 4 * q + 4, :].bitcast(I32),
                 )
-                pick_codes(a)
-            if item == "s":
-                for q in range(4):
-                    nc.sync.dma_start(
-                        tab_plane[32 * q : 32 * q + 8, :].bitcast(I32),
-                        tab_scales[:, 4 * q : 4 * q + 4, :].bitcast(I32),
-                    )
-                nc.vector.tensor_copy(v_scales[:], tab_plane[:].indirect(offsets[:]))
-            if item == "m":
-                nc.sync.dma_start(v_moved[0:112, :].bitcast(I32), v_scales[4:116, :].bitcast(I32))
-            if item[0] == "c":
-                c = int(item[1])
-                raws[c] = keep.tile([P, 4, PASS], F32, name="raw%d" % c, align_bytes=64)
-                if c < 4:
-                    b, a = divmod(c, 2)
-                    block = w2[PASS * a : PASS * (a + 1), PASS * b : PASS * (b + 1)]
-                    nc.sync.dma_start(raws[c][:], block.rearrange("(p i) c -> p i c", i=4))
-                else:
-                    b = c - 4
-                    rows = w3[PASS * b : PASS * (b + 1), :].rearrange("(m t e) n -> t m e n", t=4, e=4)
-                    for t in range(4):
-                        nc.sync.dma_start(raws[c][:, t, :], rows[t])
-            if item[0] == "g":
-                n = int(item[1])
-                volume[n] = keep.tile([P, T], F32, name="volume%d" % n)
-                nc.sync.dma_start(volume[n][:], gT[P * n : P * (n + 1), :])
-            if item == "w":
-                nc.sync.dma_start(
-                    w1_raw[:].bitcast(I32), w1_words.rearrange("a p c -> p a c").bitcast(I32)
-                )
-            if item == "x":
-                for q in range(4):
-                    nc.sync.dma_start(
-                        w1_plane[32 * q : 32 * q + 4, :, :].bitcast(I32),
-                        w1_scales[:, 4 * q : 4 * q + 4, :].rearrange("a r c -> r a c").bitcast(I32),
-                    )
+            nc.vector.tensor_copy(v_scales[:], tab_plane[:].indirect(offsets[:]))
+
+        def load_w2(b, a):
+            raws["w2", b, a] = keep.tile([P, 4, PASS], F32, name="w2_raw%d%d" % (b, a), align_bytes=64)
+            block = w2[PASS * a : PASS * (a + 1), PASS * b : PASS * (b + 1)]
+            nc.sync.dma_start(raws["w2", b, a][:], block.rearrange("(p i) c -> p i c", i=4))
+
+        def load_w3(b):
+            raws["w3", b] = keep.tile([P, 4, PASS], F32, name="w3_raw%d" % b, align_bytes=64)
+            rows = w3[PASS * b : PASS * (b + 1), :].rearrange("(m t e) n -> t m e n", t=4, e=4)
+            for t in range(4):
+                nc.sync.dma_start(raws["w3", b][:, t, :], rows[t])
+
+        gather_table(0)
+        gather_table_scales()
+        gather_table(1)
+        load_w2(0, 0)
+        load_w2(0, 1)
+        for q in range(4):
+            nc.sync.dma_start(
+                w1_plane[32 * q : 32 * q + 4, :, :].bitcast(I32),
+                w1_scales[:, 4 * q : 4 * q + 4, :].rearrange("a r c -> r a c").bitcast(I32),
+            )
+        load_w2(1, 0)
+        nc.sync.dma_start(w1_raw[:].bitcast(I32), w1_words.rearrange("a p c -> p a c").bitcast(I32))
+        nc.sync.dma_start(v_moved[0:112, :].bitcast(I32), v_scales[4:116, :].bitcast(I32))
+        load_w2(1, 1)
+        load_w3(0)
+        load_w3(1)
+        for n in range(ROW_TILES):
+            volume[n] = keep.tile([P, T], F32, name="volume%d" % n)
+            nc.sync.dma_start(volume[n][:], gT[P * n : P * (n + 1), :])
 
         w_codes, w_scales = {}, {}
 
-        def quantize_weight(c):
+        def quantize_weight(key, columns, cast):
+            name = "".join(str(part) for part in key)
             grouped = ring.tile([P, PASS, 4], BF16, name="grouped", align_bytes=64)
-            cut = ON_VECTOR[c]
-            if c < 4:
-                dst = grouped[:].rearrange("p (t m e) i -> p t m i e", t=4, e=4)
-                src = raws[c][:].rearrange("p i (m t e) -> p t m i e", t=4, e=4)
-            else:
-                dst = grouped[:].rearrange("p (t m e) i -> p t m i e", t=4, e=4)
-                src = raws[c][:].rearrange("p i (t m e) -> p t m i e", t=4, e=4)
-            w_codes[c] = keep.tile([P, PASS], U32, name="w_codes%d" % c, align_bytes=64)
-            w_scales[c] = keep.tile([P, PASS], U8, name="w_scales%d" % c, align_bytes=64)
+            dst = grouped[:].rearrange("p (t m e) i -> p t m i e", t=4, e=4)
+            src = raws[key][:].rearrange("p i (%s) -> p t m i e" % columns, t=4, e=4)
+            w_codes[key] = keep.tile([P, PASS], U32, name="codes_" + name, align_bytes=64)
+            w_scales[key] = keep.tile([P, PASS], U8, name="scales_" + name, align_bytes=64)
             for half in range(2):
-                ts = slice(2 * half, 2 * half + 2)
-                if 2 * half < cut:
-                    nc.vector.tensor_copy(dst[:, ts], src[:, ts])
-                else:
-                    nc.scalar.copy(dst[:, ts], src[:, ts])
+                cast(dst[:, 2 * half : 2 * half + 2], src[:, 2 * half : 2 * half + 2])
             for half in range(2):
                 cols = slice(2 * P * half, 2 * P * (half + 1))
                 nc.vector.quantize_mx(
-                    out=w_codes[c][:, cols].bitcast(E4M3),
-                    scales=w_scales[c][:, cols],
+                    out=w_codes[key][:, cols].bitcast(E4M3),
+                    scales=w_scales[key][:, cols],
                     in_=grouped[:, cols, :].rearrange("p c i -> p (c i)"),
                 )
 
@@ -155,9 +141,9 @@ def tile_list_cap_voxel_update_kernel(
 
         taken = {"damping": 0, "drive": 0, "change": 0}
 
-        def next_bank(stage, depth):
-            bank = psum.tile([P, PASS], F32, name="%s%d" % (stage, taken[stage] % depth))
-            taken[stage] = taken[stage] + 1
+        def next_bank(kind):
+            bank = psum.tile([P, PASS], F32, name="%s%d" % (kind, taken[kind] % BANKS[kind]))
+            taken[kind] = taken[kind] + 1
             return bank
 
         def in_word_order(bank):
@@ -166,49 +152,53 @@ def tile_list_cap_voxel_update_kernel(
         def as_words(tile):
             return tile.rearrange("p (j t) -> p j t", t=4)
 
+        def place_of(u):
+            return u // 4, u % 4 // 2, P * (u % 2)
+
+        def entries_of(u):
+            c, b, j0 = place_of(u)
+            return slice(CHUNK * c + j0, CHUNK * c + j0 + P)
+
         sizes, roots, factors = {}, {}, {}
 
         def damp(u):
-            jt, b = units[u]
-            js = slice(P * jt, P * (jt + 1))
-            bank = next_bank("damping", BANKS[0])
+            b, js = place_of(u)[1], entries_of(u)
+            bank = next_bank("damping")
             for t in range(4):
                 ts = slice(P * t, P * (t + 1))
                 for a in (1, 0):
                     nc.tensor.matmul_mx(
                         out=bank[:, ts],
-                        lhsT=w_codes[2 * b + a][:, ts].bitcast(E4M3),
-                        lhsT_scale=w_scales[2 * b + a][:, ts],
+                        lhsT=w_codes["w2", b, a][:, ts].bitcast(E4M3),
+                        lhsT_scale=w_scales["w2", b, a][:, ts],
                         rhs=v_codes[a][:, js].bitcast(E4M3),
                         rhs_scale=v_scales[4 * a :, js],
                         start=(a == 1),
                         stop=(a == 0),
                     )
-            sizes[u] = ring.tile([P, PASS], F32, name="size", bufs=SIZE_BUFS)
+            sizes[u] = ring.tile([P, PASS], F32, name="size", bufs=3)
             nc.scalar.activation(as_words(sizes[u][:]), in_word_order(bank), ACT.Abs)
 
         def root(u):
-            roots[u] = ring.tile([P, PASS], F32, name="root", bufs=ROOT_BUFS)
-            nc.scalar.activation(roots[u][:], sizes[u][:], ACT.Abs_reciprocal_sqrt, bias=ones[:, 2:3])
+            roots[u] = ring.tile([P, PASS], F32, name="root", bufs=3)
+            nc.scalar.activation(roots[u][:], sizes[u][:], ACT.Abs_reciprocal_sqrt, bias=one)
 
         def square(u):
-            factors[u] = ring.tile([P, PASS], F32, name="factor", bufs=FACTOR_BUFS)
-            if u not in TWICE:
-                nc.scalar.activation(factors[u][:], roots[u][:], ACT.Square)
+            factors[u] = ring.tile([P, PASS], F32, name="factor", bufs=4)
+            nc.scalar.activation(factors[u][:], roots[u][:], ACT.Square)
 
-        h_grouped, h_parts, plains = {}, {}, {}
+        hosts = {(0, 0): ("w2", 1, 1), (0, 1): ("w3", 1)}
+        h_grouped, h_parts, drives = {}, {}, {}
 
         def drive(u):
-            jt, b = units[u]
-            js = slice(P * jt, P * (jt + 1))
-            c, j0 = divmod(P * jt, CHUNK)
-            if (c, b) not in h_grouped:
-                if (c, b) in HOSTS:
-                    host = raws[HOSTS[c, b][0]][:].rearrange("p i c -> p (i c)").bitcast(BF16)
-                    h_grouped[c, b] = host[:, 4 * CHUNK * HOSTS[c, b][1] : 4 * CHUNK * (HOSTS[c, b][1] + 1)]
-                else:
-                    h_grouped[c, b] = ring.tile([P, 4 * CHUNK], BF16, name="h_grouped", align_bytes=64, bufs=3)[:]
-            bank = next_bank("drive", BANKS[1])
+            c, b, j0 = place_of(u)
+            js = entries_of(u)
+            if (c, b) in hosts:
+                host = raws[hosts[c, b]][:].rearrange("p i c -> p (i c)").bitcast(BF16)
+                h_grouped[c, b] = host[:, : 4 * CHUNK]
+            elif j0 == 0:
+                h_grouped[c, b] = ring.tile([P, 4 * CHUNK], BF16, name="h_grouped", align_bytes=64)[:]
+            bank = next_bank("drive")
             for t in range(4):
                 for a in range(2):
                     col = P * ((2 * a + b) * 4 + t)
@@ -221,13 +211,14 @@ def tile_list_cap_voxel_update_kernel(
                         start=(a == 0),
                         stop=(a == 1),
                     )
-            h_part = h_grouped[c, b][:, 4 * j0 : 4 * (j0 + P)]
-            h_parts[u] = h_part
-            if u in ON_GPSIMD or u in TWICE:
-                plains[u] = ring.tile([P, PASS], F32, name="plain", bufs=2)
-                nc.scalar.copy(as_words(plains[u][:]), in_word_order(bank))
+            h_parts[u] = h_grouped[c, b][:, 4 * j0 : 4 * (j0 + P)]
+            if on_gpsimd(u):
+                drives[u] = ring.tile([P, PASS], F32, name="drive", bufs=2)
+                nc.scalar.copy(as_words(drives[u][:]), in_word_order(bank))
             else:
-                nc.vector.tensor_tensor(as_words(h_part), in_word_order(bank), as_words(factors[u][:]), ALU.mult)
+                nc.vector.tensor_tensor(
+                    as_words(h_parts[u]), in_word_order(bank), as_words(factors[u][:]), ALU.mult
+                )
 
         h_codes, h_scales = {}, {}
 
@@ -241,77 +232,79 @@ def tile_list_cap_voxel_update_kernel(
         def listed(c0, c1, n):
             return volume[n][:].indirect(offsets[:, CHUNK * c0 // 16 : CHUNK * c1 // 16])
 
-        picked, totals = {}, {}
+        picked = keep.tile([P, S], F32, name="picked")
+        totals = {}
 
-        def first_half(c0, c1, n, step):
+        def add_change(c0, c1, n, step):
             ns = slice(P * n, P * (n + 1))
             width = CHUNK * (c1 - c0)
-            bank = next_bank("change", BANKS[2])[:, :width]
+            bank = next_bank("change")[:, :width]
             for c in range(c0, c1):
                 for b in (1, 0):
                     nc.tensor.matmul_mx(
                         out=bank[:, CHUNK * (c - c0) : CHUNK * (c - c0 + 1)],
-                        lhsT=w_codes[4 + b][:, ns].bitcast(E4M3),
-                        lhsT_scale=w_scales[4 + b][:, ns],
+                        lhsT=w_codes["w3", b][:, ns].bitcast(E4M3),
+                        lhsT_scale=w_scales["w3", b][:, ns],
                         rhs=h_codes[c, b][:].bitcast(E4M3),
                         rhs_scale=h_scales[c, b][:],
                         start=(b == 1),
                         stop=(b == 0),
                     )
-            total = ring.tile([P, width], F32, name="total", bufs=SUM_BUFS)
-            if n not in FUSED:
-                nc.vector.tensor_tensor(total[:], bank, picked[n][:, CHUNK * c0 : CHUNK * c1], ALU.add)
+            totals[c0, n] = ring.tile([P, width], F32, name="total", bufs=2)
+            if n == 0:
+                nc.vector.tensor_tensor(
+                    totals[c0, n][:], bank, picked[:, CHUNK * c0 : CHUNK * c1], ALU.add
+                )
             else:
-                if step in ON_GPSIMD:
+                if on_gpsimd(step):
                     change = h_parts[step].bitcast(F32)
-                elif step in TWICE:
-                    change = factors[step][:, :CHUNK]
-                elif step - 1 in TWICE:
-                    change = h_parts[step - 1].bitcast(F32)
                 else:
                     change = ring.tile([P, width], F32, name="change", bufs=2)[:]
                 nc.scalar.copy(change, bank)
-                nc.vector.tensor_tensor(total[:], listed(c0, c1, n), change, ALU.add)
-            totals[c0, n] = total
+                nc.vector.tensor_tensor(totals[c0, n][:], listed(c0, c1, n), change, ALU.add)
 
-        def second_half(c0, c1, n, step):
+        def put_back(c0, c1, n, step):
             width = CHUNK * (c1 - c0)
-            if step == len(units) - 1:
+            if step == LAST_UNIT:
                 new = factors[step][:, :width]
             else:
                 new = ring.tile([P, width], F32, name="new", bufs=2)[:]
             nc.scalar.activation(new, totals[c0, n][:], ACT.Relu)
             nc.vector.tensor_copy(listed(c0, c1, n), new)
-            if c1 == S // CHUNK:
+            if c1 == CHUNKS:
                 nc.sync.dma_start(out[P * n : P * (n + 1), :], volume[n][:])
 
-        units = [(jt, b) for c in range(S // CHUNK) for b in range(2) for jt in (2 * c, 2 * c + 1)]
-        jobs = [(c, c + 1, n) for c in range(4) for n in range(4) if c < 2 or n < 3] + [(2, 4, 3)]
-        for item in PREPARE.split():
-            if item == "w":
-                deal_w1()
-            else:
-                quantize_weight(int(item))
-        for step in range(-2 - LEAD, JOB_STEPS[-1] + 2):
-            for ahead, stage in ((2, damp), (1, root), (0, square)):
-                if 0 <= step + LEAD + ahead < len(units):
-                    stage(step + LEAD + ahead)
-            if step in W3_STEP:
-                quantize_weight(4 + W3_STEP.index(step))
-            if 0 <= step < len(units):
+        last_tile = ROW_TILES - 1
+        updates = [
+            (c, c + 1, n)
+            for c in range(CHUNKS)
+            for n in range(ROW_TILES)
+            if c < CHUNKS - 2 or n < last_tile
+        ] + [(CHUNKS - 2, CHUNKS, last_tile)]
+
+        quantize_weight(("w2", 0, 0), "m t e", nc.scalar.copy)
+        quantize_weight(("w2", 0, 1), "m t e", nc.scalar.copy)
+        quantize_weight(("w2", 1, 0), "m t e", nc.vector.tensor_copy)
+        deal_w1()
+        quantize_weight(("w2", 1, 1), "m t e", nc.vector.tensor_copy)
+
+        for step in range(-2, FIRST_UPDATE + len(updates) + 1):
+            for ahead, scalar_pass in ((2, damp), (1, root), (0, square)):
+                if 0 <= step + ahead < UNITS:
+                    scalar_pass(step + ahead)
+            if step == 2:
+                for b in range(2):
+                    quantize_weight(("w3", b), "t m e", nc.vector.tensor_copy)
+            if 0 <= step < UNITS:
                 drive(step)
             if step == 3:
-                picked[0] = keep.tile([P, S], F32, name="picked")
-                nc.vector.tensor_copy(picked[0][:], volume[0][:].indirect(offsets[:]))
-            if step in JOB_STEPS:
-                first_half(*jobs[JOB_STEPS.index(step)], step)
-            if step in ON_GPSIMD:
-                nc.gpsimd.tensor_tensor(h_parts[step], plains[step][:], factors[step][:], ALU.mult)
-            if step in TWICE:
-                nc.gpsimd.tensor_tensor(factors[step][:], plains[step][:], roots[step][:], ALU.mult)
-            if step - 1 in TWICE:
-                nc.gpsimd.tensor_tensor(h_parts[step - 1], factors[step - 1][:], roots[step - 1][:], ALU.mult)
-            if 0 <= step < len(units) and units[step][0] % 2 == 1:
-                quantize_h(units[step][0] // 2, units[step][1])
-            if step - 1 in JOB_STEPS:
-                second_half(*jobs[JOB_STEPS.index(step - 1)], step)
+                nc.vector.tensor_copy(picked[:], volume[0][:].indirect(offsets[:]))
+            k = step - FIRST_UPDATE
+            if 0 <= k < len(updates):
+                add_change(*updates[k], step)
+            if on_gpsimd(step):
+                nc.gpsimd.tensor_tensor(h_parts[step], drives[step][:], factors[step][:], ALU.mult)
+            if 0 <= step < UNITS and step % 2 == 1:
+                quantize_h(*place_of(step)[:2])
+            if 0 < k:
+                put_back(*updates[k - 1], step)

@@ -24,6 +24,7 @@ ROW_TILES = N // P
 UNITS = 4 * CHUNKS
 LAST_UNIT = UNITS - 1
 FIRST_UPDATE = 5
+AHEAD = 768
 BANKS = {"damping": 3, "drive": 3, "change": 2}
 
 
@@ -62,9 +63,13 @@ def tile_list_cap_voxel_update_kernel(
 
         def gather_table(a):
             words = keep.tile([P, T], U32, name="tab%d" % a)
-            nc.sync.dma_start(
-                words[:].bitcast(I32), tab_words[a].rearrange("p t i -> p (t i)").bitcast(I32)
-            )
+            source = tab_words[a].rearrange("p t i -> p (t i)").bitcast(I32)
+            if a == 0:
+                nc.sync.dma_start(words[:, :AHEAD].bitcast(I32), source[:, :AHEAD])
+                gather_table_scales()
+                nc.sync.dma_start(words[:, AHEAD:].bitcast(I32), source[:, AHEAD:])
+            else:
+                nc.sync.dma_start(words[:].bitcast(I32), source)
             v_codes[a] = keep.tile([P, S], U32, name="v_codes%d" % a, align_bytes=64)
             nc.vector.tensor_copy(v_codes[a][:], words[:].indirect(offsets[:]))
 
@@ -88,7 +93,6 @@ def tile_list_cap_voxel_update_kernel(
                 nc.sync.dma_start(raws["w3", b][:, t, :], rows[t])
 
         gather_table(0)
-        gather_table_scales()
         gather_table(1)
         load_w2(0, 0)
         load_w2(0, 1)
@@ -98,9 +102,9 @@ def tile_list_cap_voxel_update_kernel(
                 w1_scales[:, 4 * q : 4 * q + 4, :].rearrange("a r c -> r a c").bitcast(I32),
             )
         load_w2(1, 0)
+        load_w2(1, 1)
         nc.sync.dma_start(w1_raw[:].bitcast(I32), w1_words.rearrange("a p c -> p a c").bitcast(I32))
         nc.sync.dma_start(v_moved[0:112, :].bitcast(I32), v_scales[4:116, :].bitcast(I32))
-        load_w2(1, 1)
         load_w3(0)
         load_w3(1)
         for n in range(ROW_TILES):
@@ -117,7 +121,7 @@ def tile_list_cap_voxel_update_kernel(
             w_codes[key] = keep.tile([P, PASS], U32, name="codes_" + name, align_bytes=64)
             w_scales[key] = keep.tile([P, PASS], U8, name="scales_" + name, align_bytes=64)
             for half in range(2):
-                cast(dst[:, 2 * half : 2 * half + 2], src[:, 2 * half : 2 * half + 2])
+                cast[half](dst[:, 2 * half : 2 * half + 2], src[:, 2 * half : 2 * half + 2])
             for half in range(2):
                 cols = slice(2 * P * half, 2 * P * (half + 1))
                 nc.vector.quantize_mx(
@@ -282,11 +286,12 @@ def tile_list_cap_voxel_update_kernel(
             if c < CHUNKS - 2 or n < last_tile
         ] + [(CHUNKS - 2, CHUNKS, last_tile)]
 
-        quantize_weight(("w2", 0, 0), "m t e", nc.scalar.copy)
-        quantize_weight(("w2", 0, 1), "m t e", nc.scalar.copy)
-        quantize_weight(("w2", 1, 0), "m t e", nc.vector.tensor_copy)
+        on_scalar, on_vector = (nc.scalar.copy,) * 2, (nc.vector.tensor_copy,) * 2
+        quantize_weight(("w2", 0, 0), "m t e", on_scalar)
+        quantize_weight(("w2", 0, 1), "m t e", (nc.scalar.copy, nc.vector.tensor_copy))
+        quantize_weight(("w2", 1, 0), "m t e", on_vector)
+        quantize_weight(("w2", 1, 1), "m t e", on_vector)
         deal_w1()
-        quantize_weight(("w2", 1, 1), "m t e", nc.vector.tensor_copy)
 
         for step in range(-2, FIRST_UPDATE + len(updates) + 1):
             for ahead, scalar_pass in ((2, damp), (1, root), (0, square)):
@@ -294,7 +299,7 @@ def tile_list_cap_voxel_update_kernel(
                     scalar_pass(step + ahead)
             if step == 2:
                 for b in range(2):
-                    quantize_weight(("w3", b), "t m e", nc.vector.tensor_copy)
+                    quantize_weight(("w3", b), "t m e", on_vector)
             if 0 <= step < UNITS:
                 drive(step)
             if step == 3:

@@ -57,7 +57,7 @@ def tile_list_cap_voxel_update_kernel(
         nc.scalar.activation(ones[:, 2:3], ones[:, 1:2], ACT.Sign)
         one = ones[:, 2:3]
 
-        w1_raw = keep.tile([P, 2, 2 * H], U8, name="w1_raw", align_bytes=64)
+        w1_raw = [keep.tile([P, 2, H], U8, name="w1_raw%d" % b, align_bytes=64) for b in range(2)]
         v_scales = keep.tile([P, S], U8, name="v_scales", align_bytes=64)
         v_codes, raws, volume = {}, {}, {}
 
@@ -71,7 +71,9 @@ def tile_list_cap_voxel_update_kernel(
             else:
                 nc.sync.dma_start(words[:].bitcast(I32), source)
             v_codes[a] = keep.tile([P, S], U32, name="v_codes%d" % a, align_bytes=64)
-            nc.vector.tensor_copy(v_codes[a][:], words[:].indirect(offsets[:]))
+            cuts = (0, S) if a == 0 else (0, CHUNK, 2 * CHUNK, S)
+            for j0, j1 in zip(cuts, cuts[1:]):
+                nc.vector.tensor_copy(v_codes[a][:, j0:j1], words[:].indirect(offsets[:, j0 // 16 : j1 // 16]))
 
         def gather_table_scales():
             for q in range(4):
@@ -86,6 +88,10 @@ def tile_list_cap_voxel_update_kernel(
             block = w2[PASS * a : PASS * (a + 1), PASS * b : PASS * (b + 1)]
             nc.sync.dma_start(raws["w2", b, a][:], block.rearrange("(p i) c -> p i c", i=4))
 
+        def load_w1(b):
+            half = w1_words[:, :, H * b : H * (b + 1)].rearrange("a p c -> p a c")
+            nc.sync.dma_start(w1_raw[b][:].bitcast(I32), half.bitcast(I32))
+
         def load_w3(b):
             raws["w3", b] = keep.tile([P, 4, PASS], F32, name="w3_raw%d" % b, align_bytes=64)
             rows = w3[PASS * b : PASS * (b + 1), :].rearrange("(m t e) n -> t m e n", t=4, e=4)
@@ -93,29 +99,31 @@ def tile_list_cap_voxel_update_kernel(
                 nc.sync.dma_start(raws["w3", b][:, t, :], rows[t])
 
         gather_table(0)
-        gather_table(1)
         load_w2(0, 0)
         load_w2(0, 1)
+        gather_table(1)
         for q in range(4):
             nc.sync.dma_start(
                 w1_plane[32 * q : 32 * q + 4, :, :].bitcast(I32),
                 w1_scales[:, 4 * q : 4 * q + 4, :].rearrange("a r c -> r a c").bitcast(I32),
             )
         load_w2(1, 0)
-        load_w2(1, 1)
-        nc.sync.dma_start(w1_raw[:].bitcast(I32), w1_words.rearrange("a p c -> p a c").bitcast(I32))
+        load_w1(0)
         nc.sync.dma_start(v_moved[0:112, :].bitcast(I32), v_scales[4:116, :].bitcast(I32))
+        load_w2(1, 1)
+        load_w1(1)
         load_w3(0)
         load_w3(1)
         for n in range(ROW_TILES):
             volume[n] = keep.tile([P, T], F32, name="volume%d" % n)
             nc.sync.dma_start(volume[n][:], gT[P * n : P * (n + 1), :])
 
-        w_codes, w_scales = {}, {}
+        w_codes, w_scales, casts = {}, {}, {}
 
         def quantize_weight(key, columns, cast):
             name = "".join(str(part) for part in key)
             grouped = ring.tile([P, PASS, 4], BF16, name="grouped", align_bytes=64)
+            casts[key] = grouped
             dst = grouped[:].rearrange("p (t m e) i -> p t m i e", t=4, e=4)
             src = raws[key][:].rearrange("p i (%s) -> p t m i e" % columns, t=4, e=4)
             w_codes[key] = keep.tile([P, PASS], U32, name="codes_" + name, align_bytes=64)
@@ -130,14 +138,40 @@ def tile_list_cap_voxel_update_kernel(
                     in_=grouped[:, cols, :].rearrange("p c i -> p (c i)"),
                 )
 
-        w1_codes = keep.tile([P, 4 * H], U8, name="w1_codes", align_bytes=64)
+        def front_of_w3(b, grouped):
+            w_codes["w3", b] = keep.tile([P, PASS], U32, name="codes_w3%d" % b, align_bytes=64)
+            w_scales["w3", b] = keep.tile([P, PASS], U8, name="scales_w3%d" % b, align_bytes=64)
+            nc.vector.tensor_copy(
+                grouped.rearrange("p (g e i) -> p g i e", e=4, i=4),
+                raws["w3", b][:, :, :CHUNK].rearrange("p i (g e) -> p g i e", e=4),
+            )
+
+        def spent(b):
+            return raws["w3", 1][:, b::2, :CHUNK].bitcast(BF16)
+
+        def back_of_w3(b):
+            nc.gpsimd.tensor_scalar(
+                spent(b).rearrange("p t (c i) -> p t c i", i=4),
+                raws["w3", b][:, :, CHUNK:].rearrange("p i (t c) -> p t c i", t=2),
+                1.0, 0.0, ALU.mult, ALU.add,
+            )
+
+        def quantize_w3(b, c0, grouped):
+            cols = slice(c0, c0 + grouped.shape[1] // 4)
+            nc.vector.quantize_mx(out=w_codes["w3", b][:, cols].bitcast(E4M3), scales=w_scales["w3", b][:, cols], in_=grouped)
+
+        w3_front = keep.tile([P, 8 * CHUNK], BF16, name="w3_front", align_bytes=64)
+
+        w1_codes = [keep.tile([P, 2 * H], U8, name="w1_codes%d" % b, align_bytes=64) for b in range(2)]
         w1_dealt = keep.tile([P, 2 * H], U8, name="w1_dealt", align_bytes=64)
 
-        def deal_w1():
+        def deal_codes(b):
             nc.vector.tensor_copy(
-                w1_codes[:].bitcast(I32).rearrange("p (g t m w) -> p g t m w", g=4, t=4, w=2),
-                w1_raw[:].bitcast(I32).rearrange("p a (b m t w) -> p (a b) t m w", b=2, t=4, w=2),
+                w1_codes[b][:].bitcast(I32).rearrange("p (a t m w) -> p a t m w", a=2, t=4, w=2),
+                w1_raw[b][:].bitcast(I32).rearrange("p a (m t w) -> p a t m w", t=4, w=2),
             )
+
+        def deal_scales():
             nc.vector.tensor_copy(
                 w1_dealt[:].bitcast(I32).rearrange("p (g t m) -> p g t m", g=4, t=4),
                 w1_plane[:].bitcast(I32).rearrange("p a (b m t) -> p (a b) t m", b=2, t=4),
@@ -167,31 +201,41 @@ def tile_list_cap_voxel_update_kernel(
 
         def damp(u):
             b, js = place_of(u)[1], entries_of(u)
-            bank = next_bank("damping")
-            for t in range(4):
-                ts = slice(P * t, P * (t + 1))
-                for a in (1, 0):
+            if u in (4, 5):
+                bank = next_bank("change")
+            else:
+                bank = psum.tile([P, PASS], F32, name="damping%d" % (u % 3 if u < 4 else 1 + u % 2))
+            for a in range(2):
+                for t in range(4):
+                    ts = slice(P * t, P * (t + 1))
                     nc.tensor.matmul_mx(
                         out=bank[:, ts],
                         lhsT=w_codes["w2", b, a][:, ts].bitcast(E4M3),
                         lhsT_scale=w_scales["w2", b, a][:, ts],
                         rhs=v_codes[a][:, js].bitcast(E4M3),
                         rhs_scale=v_scales[4 * a :, js],
-                        start=(a == 1),
-                        stop=(a == 0),
+                        start=(a, t) == (0, 0),
+                        stop=(a, t) == (1, 3),
                     )
-            sizes[u] = ring.tile([P, PASS], F32, name="size", bufs=3)
+            if u in (6, 7):
+                sizes[u] = factors[u - 4]
+            else:
+                sizes[u] = ring.tile([P, PASS], F32, name="early_size" if u in (4, 5) else "size", bufs=2 if u in (4, 5) else 3)
             nc.scalar.activation(as_words(sizes[u][:]), in_word_order(bank), ACT.Abs)
 
         def root(u):
-            roots[u] = ring.tile([P, PASS], F32, name="root", bufs=3)
+            roots[u] = ring.tile([P, PASS], F32, name="early_root" if u == 4 else "root", bufs=1 if u == 4 else 3)
             nc.scalar.activation(roots[u][:], sizes[u][:], ACT.Abs_reciprocal_sqrt, bias=one)
 
         def square(u):
+            if u == 4:
+                factors[u] = casts["w2", 1, 1][:, CHUNK:, :].rearrange("p c i -> p (c i)").bitcast(F32)
+                nc.gpsimd.tensor_tensor(factors[u], roots[u][:], roots[u][:], ALU.mult)
+                return
             factors[u] = ring.tile([P, PASS], F32, name="factor", bufs=4)
             nc.scalar.activation(factors[u][:], roots[u][:], ACT.Square)
 
-        hosts = {(0, 0): ("w2", 1, 1), (0, 1): ("w3", 1)}
+        hosts = {(0, 0): ("w2", 1, 1)}
         h_grouped, h_parts, drives = {}, {}, {}
 
         def drive(u):
@@ -200,22 +244,27 @@ def tile_list_cap_voxel_update_kernel(
             if (c, b) in hosts:
                 host = raws[hosts[c, b]][:].rearrange("p i c -> p (i c)").bitcast(BF16)
                 h_grouped[c, b] = host[:, : 4 * CHUNK]
-            elif j0 == 0:
-                h_grouped[c, b] = ring.tile([P, 4 * CHUNK], BF16, name="h_grouped", align_bytes=64)[:]
+            elif (c, b) == (1, 0):
+                h_grouped[c, b] = w3_front[:, 2 * CHUNK : 6 * CHUNK]
+            elif j0 == 0 and c > 0:
+                h_grouped[c, b] = ring.tile([P, 4 * CHUNK], BF16, name="h_grouped", align_bytes=64, bufs=4)[:]
             bank = next_bank("drive")
             for t in range(4):
                 for a in range(2):
                     col = P * ((2 * a + b) * 4 + t)
                     nc.tensor.matmul_mx(
                         out=bank[:, P * t : P * (t + 1)],
-                        lhsT=w1_codes[:, 2 * col : 2 * (col + P)].bitcast(E2M1),
+                        lhsT=w1_codes[b][:, 2 * P * (4 * a + t) : 2 * P * (4 * a + t + 1)].bitcast(E2M1),
                         lhsT_scale=w1_dealt[:, col : col + P],
                         rhs=v_codes[a][:, js].bitcast(E4M3),
                         rhs_scale=(v_scales, v_moved)[a][:, js],
                         start=(a == 0),
                         stop=(a == 1),
                     )
-            h_parts[u] = h_grouped[c, b][:, 4 * j0 : 4 * (j0 + P)]
+            if (c, b) == (0, 1):
+                h_parts[u] = raws["w3", 1][:, u % 2, :CHUNK].bitcast(BF16)
+            else:
+                h_parts[u] = h_grouped[c, b][:, 4 * j0 : 4 * (j0 + P)]
             if on_gpsimd(u):
                 drives[u] = ring.tile([P, PASS], F32, name="drive", bufs=2)
                 nc.scalar.copy(as_words(drives[u][:]), in_word_order(bank))
@@ -229,6 +278,11 @@ def tile_list_cap_voxel_update_kernel(
         def quantize_h(c, b):
             h_codes[c, b] = keep.tile([P, CHUNK], U32, name="h_codes%d%d" % (c, b), align_bytes=64)
             h_scales[c, b] = keep.tile([P, CHUNK], U8, name="h_scales%d%d" % (c, b), align_bytes=64)
+            if (c, b) == (0, 1):
+                for u in (2, 3):
+                    js = slice(P * (u % 2), P * (u % 2 + 1))
+                    nc.vector.quantize_mx(out=h_codes[c, b][:, js].bitcast(E4M3), scales=h_scales[c, b][:, js], in_=h_parts[u])
+                return
             nc.vector.quantize_mx(
                 out=h_codes[c, b][:].bitcast(E4M3), scales=h_scales[c, b][:], in_=h_grouped[c, b]
             )
@@ -289,27 +343,50 @@ def tile_list_cap_voxel_update_kernel(
         on_scalar, on_vector = (nc.scalar.copy,) * 2, (nc.vector.tensor_copy,) * 2
         quantize_weight(("w2", 0, 0), "m t e", on_scalar)
         quantize_weight(("w2", 0, 1), "m t e", (nc.scalar.copy, nc.vector.tensor_copy))
+        deal_scales()
         quantize_weight(("w2", 1, 0), "m t e", on_vector)
+        deal_codes(0)
         quantize_weight(("w2", 1, 1), "m t e", on_vector)
-        deal_w1()
+        deal_codes(1)
 
-        for step in range(-2, FIRST_UPDATE + len(updates) + 1):
-            for ahead, scalar_pass in ((2, damp), (1, root), (0, square)):
-                if 0 <= step + ahead < UNITS:
-                    scalar_pass(step + ahead)
+        passes = [
+            (scalar_pass, u + ahead)
+            for u in range(-2, UNITS)
+            for ahead, scalar_pass in ((2, damp), (1, root), (0, square))
+            if 0 <= u + ahead < UNITS and not (scalar_pass is square and u in (10, 12))
+        ]
+        done = 0
+        for step in range(FIRST_UPDATE + len(updates) + 1):
+            due = 3 * step + 6 - (step >= 10) - (step >= 12)
+            for scalar_pass, u in passes[done:due]:
+                scalar_pass(u)
+            done = due
             if step == 2:
-                for b in range(2):
-                    quantize_weight(("w3", b), "t m e", on_vector)
+                front_of_w3(0, w3_front[:, : 4 * CHUNK])
+                quantize_h(0, 0)
+                quantize_w3(0, 0, w3_front[:, : 4 * CHUNK])
+                front_of_w3(1, w3_front[:, 4 * CHUNK :])
             if 0 <= step < UNITS:
                 drive(step)
             if step == 3:
+                quantize_w3(1, 0, w3_front[:, 4 * CHUNK :])
+                quantize_h(0, 1)
                 nc.vector.tensor_copy(picked[:], volume[0][:].indirect(offsets[:]))
+                for b in range(2):
+                    back_of_w3(b)
+            if step == 5:
+                for b in range(2):
+                    for t in range(2):
+                        quantize_w3(b, CHUNK + P * t, spent(b)[:, t, :])
             k = step - FIRST_UPDATE
             if 0 <= k < len(updates):
                 add_change(*updates[k], step)
             if on_gpsimd(step):
                 nc.gpsimd.tensor_tensor(h_parts[step], drives[step][:], factors[step][:], ALU.mult)
-            if 0 <= step < UNITS and step % 2 == 1:
+            if 3 < step < UNITS and step % 2 == 1:
                 quantize_h(*place_of(step)[:2])
+                if step in (9, 11):
+                    factors[step + 1] = h_grouped[place_of(step)[:2]].bitcast(F32)
+                    nc.gpsimd.tensor_tensor(factors[step + 1], roots[step + 1][:], roots[step + 1][:], ALU.mult)
             if 0 < k:
                 put_back(*updates[k - 1], step)

@@ -150,10 +150,9 @@ def tile_list_cap_voxel_update_kernel(
             return raws["w3", 1][:, b::2, :CHUNK].bitcast(BF16)
 
         def back_of_w3(b):
-            nc.gpsimd.tensor_scalar(
-                spent(b).rearrange("p t (c i) -> p t c i", i=4),
-                raws["w3", b][:, :, CHUNK:].rearrange("p i (t c) -> p t c i", t=2),
-                1.0, 0.0, ALU.mult, ALU.add,
+            nc.vector.tensor_copy(
+                spent(b).rearrange("p t (g e i) -> p t g i e", e=4, i=4),
+                raws["w3", b][:, :, CHUNK:].rearrange("p i (t g e) -> p t g i e", t=2, e=4),
             )
 
         def quantize_w3(b, c0, grouped):

@@ -147,18 +147,28 @@ def tile_list_cap_voxel_update_kernel(
             )
 
         def spent(b):
-            return raws["w3", 1][:, b::2, :CHUNK].bitcast(BF16)
+            if b == 0:
+                return w3_back[:]
+            return raws["w3", 1][:, 0:2, :CHUNK].bitcast(BF16)
 
         def back_of_w3(b):
-            nc.vector.tensor_copy(
-                spent(b).rearrange("p t (g e i) -> p t g i e", e=4, i=4),
-                raws["w3", b][:, :, CHUNK:].rearrange("p i (t g e) -> p t g i e", t=2, e=4),
-            )
+            if b == 0:
+                nc.scalar.copy(
+                    spent(b).rearrange("p t (g e i) -> p t g i e", e=4, i=4),
+                    raws["w3", b][:, :, CHUNK:].rearrange("p i (t g e) -> p t g i e", t=2, e=4),
+                )
+            else:
+                nc.gpsimd.tensor_scalar(
+                    spent(b).rearrange("p t (c i) -> p t c i", i=4),
+                    raws["w3", b][:, :, CHUNK:].rearrange("p i (t c) -> p t c i", t=2),
+                    1.0, 0.0, ALU.mult, ALU.add,
+                )
 
         def quantize_w3(b, c0, grouped):
             cols = slice(c0, c0 + grouped.shape[1] // 4)
             nc.vector.quantize_mx(out=w_codes["w3", b][:, cols].bitcast(E4M3), scales=w_scales["w3", b][:, cols], in_=grouped)
 
+        w3_back = keep.tile([P, 2, 2 * CHUNK], BF16, name="w3_back", align_bytes=64)
         w3_front = keep.tile([P, 8 * CHUNK], BF16, name="w3_front", align_bytes=64)
 
         w1_codes = [keep.tile([P, 2 * H], U8, name="w1_codes%d" % b, align_bytes=64) for b in range(2)]
@@ -229,7 +239,7 @@ def tile_list_cap_voxel_update_kernel(
         def square(u):
             if u == 4:
                 factors[u] = casts["w2", 1, 1][:, CHUNK:, :].rearrange("p c i -> p (c i)").bitcast(F32)
-                nc.gpsimd.tensor_tensor(factors[u], roots[u][:], roots[u][:], ALU.mult)
+                nc.scalar.activation(factors[u], roots[u][:], ACT.Square)
                 return
             factors[u] = ring.tile([P, PASS], F32, name="factor", bufs=4)
             nc.scalar.activation(factors[u][:], roots[u][:], ACT.Square)
@@ -352,11 +362,11 @@ def tile_list_cap_voxel_update_kernel(
             (scalar_pass, u + ahead)
             for u in range(-2, UNITS)
             for ahead, scalar_pass in ((2, damp), (1, root), (0, square))
-            if 0 <= u + ahead < UNITS and not (scalar_pass is square and u in (10, 12))
+            if 0 <= u + ahead < UNITS
         ]
         done = 0
         for step in range(FIRST_UPDATE + len(updates) + 1):
-            due = 3 * step + 6 - (step >= 10) - (step >= 12)
+            due = 3 * step + 6
             for scalar_pass, u in passes[done:due]:
                 scalar_pass(u)
             done = due
@@ -384,8 +394,5 @@ def tile_list_cap_voxel_update_kernel(
                 nc.gpsimd.tensor_tensor(h_parts[step], drives[step][:], factors[step][:], ALU.mult)
             if 3 < step < UNITS and step % 2 == 1:
                 quantize_h(*place_of(step)[:2])
-                if step in (9, 11):
-                    factors[step + 1] = h_grouped[place_of(step)[:2]].bitcast(F32)
-                    nc.gpsimd.tensor_tensor(factors[step + 1], roots[step + 1][:], roots[step + 1][:], ALU.mult)
             if 0 < k:
                 put_back(*updates[k - 1], step)

@@ -84,6 +84,13 @@ def tile_list_cap_voxel_update_kernel(
             nc.vector.tensor_copy(v_scales[:], tab_plane[:].indirect(offsets[:]))
 
         def load_w2(b, a):
+            if (b, a) == (1, 1):
+                for half in range(2):
+                    key = ("w2", b, a) + (half,) * (1 - half)
+                    raws[key] = keep.tile([P, 4, CHUNK], F32, name="w2_last%d" % half, align_bytes=64)
+                    c0 = PASS * b + CHUNK * half
+                    nc.sync.dma_start(raws[key][:], w2[PASS * a :, c0 : c0 + CHUNK].rearrange("(p i) c -> p i c", i=4))
+                return
             raws["w2", b, a] = keep.tile([P, 4, PASS], F32, name="w2_raw%d%d" % (b, a), align_bytes=64)
             block = w2[PASS * a : PASS * (a + 1), PASS * b : PASS * (b + 1)]
             nc.sync.dma_start(raws["w2", b, a][:], block.rearrange("(p i) c -> p i c", i=4))
@@ -109,7 +116,10 @@ def tile_list_cap_voxel_update_kernel(
             )
         load_w2(1, 0)
         load_w1(0)
-        nc.sync.dma_start(v_moved[0:112, :].bitcast(I32), v_scales[4:116, :].bitcast(I32))
+        for q in range(4):
+            nc.sync.dma_start(
+                v_moved[32 * q : 32 * q + 4, :].bitcast(I32), v_scales[32 * q + 4 : 32 * q + 8, :].bitcast(I32)
+            )
         load_w2(1, 1)
         load_w1(1)
         load_w3(0)
@@ -129,7 +139,11 @@ def tile_list_cap_voxel_update_kernel(
             w_codes[key] = keep.tile([P, PASS], U32, name="codes_" + name, align_bytes=64)
             w_scales[key] = keep.tile([P, PASS], U8, name="scales_" + name, align_bytes=64)
             for half in range(2):
-                cast[half](dst[:, 2 * half : 2 * half + 2], src[:, 2 * half : 2 * half + 2])
+                if key == ("w2", 1, 1):
+                    src = raws[key + (half,) * (1 - half)][:].rearrange("p i (m t e) -> p t m i e", t=4, e=4)
+                    cast[half](dst[:, :, 16 * half : 16 * half + 16], src)
+                else:
+                    cast[half](dst[:, 2 * half : 2 * half + 2], src[:, 2 * half : 2 * half + 2])
             for half in range(2):
                 cols = slice(2 * P * half, 2 * P * (half + 1))
                 nc.vector.quantize_mx(

@@ -247,7 +247,7 @@ def tile_list_cap_voxel_update_kernel(
             nc.scalar.activation(as_words(sizes[u][:]), in_word_order(bank), ACT.Abs)
 
         def root(u):
-            roots[u] = ring.tile([P, PASS], F32, name="early_root" if u == 4 else "root", bufs=1 if u == 4 else 3)
+            roots[u] = ring.tile([P, PASS], F32, name="early_root" if u in (4, 5) else "root", bufs=2 if u in (4, 5) else 3)
             nc.scalar.activation(roots[u][:], sizes[u][:], ACT.Abs_reciprocal_sqrt, bias=one)
 
         def square(u):
@@ -353,7 +353,10 @@ def tile_list_cap_voxel_update_kernel(
             nc.scalar.activation(new, totals[c0, n][:], ACT.Relu)
             nc.vector.tensor_copy(listed(c0, c1, n), new)
             if c1 == CHUNKS:
-                nc.sync.dma_start(out[P * n : P * (n + 1), :], volume[n][:])
+                pieces = 2 if n == ROW_TILES - 1 else 1
+                for i in range(pieces):
+                    cols = slice(T // pieces * i, T // pieces * (i + 1))
+                    nc.sync.dma_start(out[P * n : P * (n + 1), cols], volume[n][:, cols])
 
         last_tile = ROW_TILES - 1
         updates = [

@@ -24,7 +24,6 @@ ROW_TILES = N // P
 UNITS = 4 * CHUNKS
 LAST_UNIT = UNITS - 1
 FIRST_UPDATE = 5
-AHEAD = 768
 BANKS = {"damping": 3, "drive": 3, "change": 2}
 
 
@@ -46,8 +45,10 @@ def tile_list_cap_voxel_update_kernel(
 
         tab_plane = keep.tile([P, T], U8, name="tab_plane", align_bytes=64)
         w1_plane = keep.tile([P, 2, H], U8, name="w1_plane", align_bytes=64)
-        v_moved = keep.tile([P, S], U8, name="v_moved", align_bytes=64)
-        nc.gpsimd.memset(tab_plane[:].bitcast(I32), 0)
+        v_moved = keep.tile([P, 2, S], U8, name="v_moved", align_bytes=64)
+        nc.sync.dma_start(tab_plane[:32, :].bitcast(I32), tab_scales.rearrange("a r c -> r a c").bitcast(I32))
+        nc.gpsimd.memset(tab_plane[32:64, :].bitcast(I32), 0)
+        nc.vector.memset(tab_plane[64:, :].bitcast(I32), 0)
         nc.vector.memset(w1_plane[:].bitcast(I32), 0)
         nc.vector.memset(v_moved[:].bitcast(I32), 0)
 
@@ -64,24 +65,11 @@ def tile_list_cap_voxel_update_kernel(
         def gather_table(a):
             words = keep.tile([P, T], U32, name="tab%d" % a)
             source = tab_words[a].rearrange("p t i -> p (t i)").bitcast(I32)
-            if a == 0:
-                nc.sync.dma_start(words[:, :AHEAD].bitcast(I32), source[:, :AHEAD])
-                gather_table_scales()
-                nc.sync.dma_start(words[:, AHEAD:].bitcast(I32), source[:, AHEAD:])
-            else:
-                nc.sync.dma_start(words[:].bitcast(I32), source)
+            nc.sync.dma_start(words[:].bitcast(I32), source)
             v_codes[a] = keep.tile([P, S], U32, name="v_codes%d" % a, align_bytes=64)
             cuts = (0, S) if a == 0 else (0, CHUNK, 2 * CHUNK, S)
             for j0, j1 in zip(cuts, cuts[1:]):
                 nc.vector.tensor_copy(v_codes[a][:, j0:j1], words[:].indirect(offsets[:, j0 // 16 : j1 // 16]))
-
-        def gather_table_scales():
-            for q in range(4):
-                nc.sync.dma_start(
-                    tab_plane[32 * q : 32 * q + 8, :].bitcast(I32),
-                    tab_scales[:, 4 * q : 4 * q + 4, :].bitcast(I32),
-                )
-            nc.vector.tensor_copy(v_scales[:], tab_plane[:].indirect(offsets[:]))
 
         def load_w2(b, a):
             if (b, a) == (1, 1):
@@ -105,21 +93,20 @@ def tile_list_cap_voxel_update_kernel(
             for t in range(4):
                 nc.sync.dma_start(raws["w3", b][:, t, :], rows[t])
 
+        nc.vector.tensor_copy(v_scales[:], tab_plane[:].indirect(offsets[:]))
         gather_table(0)
         load_w2(0, 0)
         load_w2(0, 1)
+        for q in range(4):
+            nc.sync.dma_start(v_moved[32 * q : 32 * q + 4, :, :].bitcast(I32), v_scales[8 * q : 8 * q + 8, :].bitcast(I32))
         gather_table(1)
+        load_w2(1, 0)
         for q in range(4):
             nc.sync.dma_start(
                 w1_plane[32 * q : 32 * q + 4, :, :].bitcast(I32),
                 w1_scales[:, 4 * q : 4 * q + 4, :].rearrange("a r c -> r a c").bitcast(I32),
             )
-        load_w2(1, 0)
         load_w1(0)
-        for q in range(4):
-            nc.sync.dma_start(
-                v_moved[32 * q : 32 * q + 4, :].bitcast(I32), v_scales[32 * q + 4 : 32 * q + 8, :].bitcast(I32)
-            )
         load_w2(1, 1)
         load_w1(1)
         load_w3(0)
@@ -236,7 +223,7 @@ def tile_list_cap_voxel_update_kernel(
                         lhsT=w_codes["w2", b, a][:, ts].bitcast(E4M3),
                         lhsT_scale=w_scales["w2", b, a][:, ts],
                         rhs=v_codes[a][:, js].bitcast(E4M3),
-                        rhs_scale=v_scales[4 * a :, js],
+                        rhs_scale=v_moved[:, a, js],
                         start=(a, t) == (0, 0),
                         stop=(a, t) == (1, 3),
                     )
@@ -280,7 +267,7 @@ def tile_list_cap_voxel_update_kernel(
                         lhsT=w1_codes[b][:, 2 * P * (4 * a + t) : 2 * P * (4 * a + t + 1)].bitcast(E2M1),
                         lhsT_scale=w1_dealt[:, col : col + P],
                         rhs=v_codes[a][:, js].bitcast(E4M3),
-                        rhs_scale=(v_scales, v_moved)[a][:, js],
+                        rhs_scale=v_moved[:, a, js],
                         start=(a == 0),
                         stop=(a == 1),
                     )

@@ -177,14 +177,14 @@ def tile_list_cap_voxel_update_kernel(
 
         def deal_codes(b):
             nc.vector.tensor_copy(
-                w1_codes[b][:].bitcast(I32).rearrange("p (a t m w) -> p a t m w", a=2, t=4, w=2),
-                w1_raw[b][:].bitcast(I32).rearrange("p a (m t w) -> p a t m w", t=4, w=2),
+                w1_codes[b][:].bitcast(I32).rearrange("p (a t m w) -> p a m t w", a=2, t=4, w=2),
+                w1_raw[b][:].bitcast(I32).rearrange("p a (m t w) -> p a m t w", t=4, w=2),
             )
 
         def deal_scales():
             nc.vector.tensor_copy(
-                w1_dealt[:].bitcast(I32).rearrange("p (g t m) -> p g t m", g=4, t=4),
-                w1_plane[:].bitcast(I32).rearrange("p a (b m t) -> p (a b) t m", b=2, t=4),
+                w1_dealt[:].bitcast(I32).rearrange("p (g t m) -> p g m t", g=4, t=4),
+                w1_plane[:].bitcast(I32).rearrange("p a (b m t) -> p (a b) m t", b=2, t=4),
             )
 
         taken = {"damping": 0, "drive": 0, "change": 0}

@@ -154,7 +154,7 @@ def tile_list_cap_voxel_update_kernel(
 
         def back_of_w3(b):
             if b == 0:
-                nc.scalar.copy(
+                nc.vector.tensor_copy(
                     spent(b).rearrange("p t (g e i) -> p t g i e", e=4, i=4),
                     raws["w3", b][:, :, CHUNK:].rearrange("p i (t g e) -> p t g i e", t=2, e=4),
                 )

@@ -242,7 +242,10 @@ def tile_list_cap_voxel_update_kernel(
                 factors[u] = casts["w2", 1, 1][:, CHUNK:, :].rearrange("p c i -> p (c i)").bitcast(F32)
                 nc.scalar.activation(factors[u], roots[u][:], ACT.Square)
                 return
-            factors[u] = ring.tile([P, PASS], F32, name="factor", bufs=4)
+            if u == 5:
+                factors[u] = keep.tile([P, PASS], F32, name="early_factor")
+            else:
+                factors[u] = ring.tile([P, PASS], F32, name="factor", bufs=4)
             nc.scalar.activation(factors[u][:], roots[u][:], ACT.Square)
 
         hosts = {(0, 0): ("w2", 1, 1)}
@@ -255,10 +258,10 @@ def tile_list_cap_voxel_update_kernel(
                 host = raws[hosts[c, b]][:].rearrange("p i c -> p (i c)").bitcast(BF16)
                 h_grouped[c, b] = host[:, : 4 * CHUNK]
             elif (c, b) == (1, 0):
-                h_grouped[c, b] = w3_front[:, 2 * CHUNK : 6 * CHUNK]
+                h_grouped[c, b] = w3_front[:, : 4 * CHUNK]
             elif j0 == 0 and c > 0:
                 h_grouped[c, b] = ring.tile([P, 4 * CHUNK], BF16, name="h_grouped", align_bytes=64, bufs=4)[:]
-            bank = next_bank("drive")
+            bank = next_bank("change" if u == 5 else "drive")
             for t in range(4):
                 for a in range(2):
                     col = P * ((2 * a + b) * 4 + t)

@@ -152,12 +152,18 @@ def tile_list_cap_voxel_update_kernel(
                 return w3_back[:]
             return raws["w3", 1][:, 0:2, :CHUNK].bitcast(BF16)
 
+        def back_piece(b, t):
+            if (b, t) == (0, 1):
+                return roots[3][:, :CHUNK].bitcast(BF16)
+            return spent(b)[:, t, :]
+
         def back_of_w3(b):
             if b == 0:
-                nc.vector.tensor_copy(
-                    spent(b).rearrange("p t (g e i) -> p t g i e", e=4, i=4),
-                    raws["w3", b][:, :, CHUNK:].rearrange("p i (t g e) -> p t g i e", t=2, e=4),
-                )
+                for t, cast in enumerate((nc.vector.tensor_copy, nc.scalar.copy)):
+                    cast(
+                        back_piece(b, t).rearrange("p (g e i) -> p g i e", e=4, i=4),
+                        raws["w3", b][:, :, CHUNK + P * t : CHUNK + P * (t + 1)].rearrange("p i (g e) -> p g i e", e=4),
+                    )
             else:
                 nc.gpsimd.tensor_scalar(
                     spent(b).rearrange("p t (c i) -> p t c i", i=4),
@@ -234,7 +240,7 @@ def tile_list_cap_voxel_update_kernel(
             nc.scalar.activation(as_words(sizes[u][:]), in_word_order(bank), ACT.Abs)
 
         def root(u):
-            roots[u] = ring.tile([P, PASS], F32, name="early_root" if u in (4, 5) else "root", bufs=2 if u in (4, 5) else 3)
+            roots[u] = ring.tile([P, PASS], F32, name="early_root" if u in (4, 5) else "root", bufs=2 if u in (4, 5) else 3, align_bytes=64)
             nc.scalar.activation(roots[u][:], sizes[u][:], ACT.Abs_reciprocal_sqrt, bias=one)
 
         def square(u):
@@ -393,7 +399,7 @@ def tile_list_cap_voxel_update_kernel(
             if step == 5:
                 for b in range(2):
                     for t in range(2):
-                        quantize_w3(b, CHUNK + P * t, spent(b)[:, t, :])
+                        quantize_w3(b, CHUNK + P * t, back_piece(b, t))
             k = step - FIRST_UPDATE
             if 0 <= k < len(updates):
                 add_change(*updates[k], step)

from contextlib import ExitStack

import concourse.mybir as mybir

K, H, N, T, S = 1024, 1024, 512, 2048, 1024
FLOPS = 2 * S * (2 * K * H + H * N)

F32 = mybir.dt.float32
BF16 = mybir.dt.bfloat16
I32 = mybir.dt.int32
U32 = mybir.dt.uint32
U16 = mybir.dt.uint16
U8 = mybir.dt.uint8
E4M3 = mybir.dt.float8_e4m3fn_x4
E2M1 = mybir.dt.float4_e2m1fn_x4
ACT = mybir.ActivationFunctionType
ALU = mybir.AluOpType

P = 128
PASS = 512
CHUNK = 256
CHUNKS = S // CHUNK
ROW_TILES = N // P
UNITS = 4 * CHUNKS
LAST_UNIT = UNITS - 1
FIRST_UPDATE = 5
BANKS = {"damping": 3, "drive": 3, "change": 2}


def on_gpsimd(u):
    return FIRST_UPDATE < u < LAST_UNIT and (u % 2 == 0 or u == LAST_UNIT - 2)


def tile_list_cap_voxel_update_kernel(
    tc, tab_words, tab_scales, w1_words, w1_scales, w2, w3, gT, offs, out
):
    nc = tc.nc
    with ExitStack() as ctx:
        keep = ctx.enter_context(tc.tile_pool(name="keep", bufs=1))
        ring = ctx.enter_context(tc.tile_pool(name="ring", bufs=3))
        psum = ctx.enter_context(tc.psum_pool(name="psum", bufs=1))

        offsets = keep.tile([P, S // 16], U16, name="offsets")
        nc.sync.dma_start(offsets[:], offs)

        tab_plane = keep.tile([P, T], U8, name="tab_plane", align_bytes=64)
        w1_plane = keep.tile([P, 2, H], U8, name="w1_plane", align_bytes=64)
        v_moved = keep.tile([P, 2, S], U8, name="v_moved", align_bytes=64)
        nc.sync.dma_start(tab_plane[:32, :].bitcast(I32), tab_scales.rearrange("a r c -> r a c").bitcast(I32))
        nc.gpsimd.memset(tab_plane[32:64, :].bitcast(I32), 0)
        nc.vector.memset(tab_plane[64:, :].bitcast(I32), 0)
        nc.vector.memset(w1_plane[:].bitcast(I32), 0)
        nc.vector.memset(v_moved[:].bitcast(I32), 0)

        ones = keep.tile([P, 3], F32, name="ones")
        nc.vector.memset(ones[:, 0:1], 1.0)
        nc.scalar.activation(ones[:, 1:2], ones[:, 0:1], ACT.Abs_reciprocal_sqrt)
        nc.scalar.activation(ones[:, 2:3], ones[:, 1:2], ACT.Sign)
        one = ones[:, 2:3]

        w1_raw = [keep.tile([P, 2, H], U8, name="w1_raw%d" % b, align_bytes=64) for b in range(2)]
        v_scales = keep.tile([P, S], U8, name="v_scales", align_bytes=64)
        v_codes, raws, volume = {}, {}, {}

        def gather_table(a):
            words = keep.tile([P, T], U32, name="tab%d" % a)
            source = tab_words[a].rearrange("p t i -> p (t i)").bitcast(I32)
            nc.sync.dma_start(words[:].bitcast(I32), source)
            v_codes[a] = keep.tile([P, S], U32, name="v_codes%d" % a, align_bytes=64)
            cuts = (0, S) if a == 0 else (0, CHUNK, 2 * CHUNK, S)
            for j0, j1 in zip(cuts, cuts[1:]):
                nc.vector.tensor_copy(v_codes[a][:, j0:j1], words[:].indirect(offsets[:, j0 // 16 : j1 // 16]))

        def load_w2(b, a):
            if (b, a) == (1, 1):
                for half in range(2):
                    key = ("w2", b, a) + (half,) * (1 - half)
                    raws[key] = keep.tile([P, 4, CHUNK], F32, name="w2_last%d" % half, align_bytes=64)
                    c0 = PASS * b + CHUNK * half
                    nc.sync.dma_start(raws[key][:], w2[PASS * a :, c0 : c0 + CHUNK].rearrange("(p i) c -> p i c", i=4))
                return
            raws["w2", b, a] = keep.tile([P, 4, PASS], F32, name="w2_raw%d%d" % (b, a), align_bytes=64)
            block = w2[PASS * a : PASS * (a + 1), PASS * b : PASS * (b + 1)]
            nc.sync.dma_start(raws["w2", b, a][:], block.rearrange("(p i) c -> p i c", i=4))

        def load_w1(b):
            half = w1_words[:, :, H * b : H * (b + 1)].rearrange("a p c -> p a c")
            nc.sync.dma_start(w1_raw[b][:].bitcast(I32), half.bitcast(I32))

        def load_w3(b):
            raws["w3", b] = keep.tile([P, 4, PASS], F32, name="w3_raw%d" % b, align_bytes=64)
            rows = w3[PASS * b : PASS * (b + 1), :].rearrange("(m t e) n -> t m e n", t=4, e=4)
            for t in range(4):
                nc.sync.dma_start(raws["w3", b][:, t, :], rows[t])

        nc.vector.tensor_copy(v_scales[:], tab_plane[:].indirect(offsets[:]))
        gather_table(0)
        load_w2(0, 0)
        load_w2(0, 1)
        for q in range(4):
            nc.sync.dma_start(v_moved[32 * q : 32 * q + 4, :, :].bitcast(I32), v_scales[8 * q : 8 * q + 8, :].bitcast(I32))
        gather_table(1)
        load_w2(1, 0)
        for q in range(4):
            nc.sync.dma_start(
                w1_plane[32 * q : 32 * q + 4, :, :].bitcast(I32),
                w1_scales[:, 4 * q : 4 * q + 4, :].rearrange("a r c -> r a c").bitcast(I32),
            )
        load_w1(0)
        load_w2(1, 1)
        load_w1(1)
        load_w3(0)
        load_w3(1)
        for n in range(ROW_TILES):
            volume[n] = keep.tile([P, T], F32, name="volume%d" % n)
            nc.sync.dma_start(volume[n][:], gT[P * n : P * (n + 1), :])

        w_codes, w_scales, casts = {}, {}, {}

        def quantize_weight(key, columns, cast):
            name = "".join(str(part) for part in key)
            grouped = ring.tile([P, PASS, 4], BF16, name="grouped", align_bytes=64)
            casts[key] = grouped
            dst = grouped[:].rearrange("p (t m e) i -> p t m i e", t=4, e=4)
            src = raws[key][:].rearrange("p i (%s) -> p t m i e" % columns, t=4, e=4)
            w_codes[key] = keep.tile([P, PASS], U32, name="codes_" + name, align_bytes=64)
            w_scales[key] = keep.tile([P, PASS], U8, name="scales_" + name, align_bytes=64)
            for half in range(2):
                if key == ("w2", 1, 1):
                    src = raws[key + (half,) * (1 - half)][:].rearrange("p i (m t e) -> p t m i e", t=4, e=4)
                    cast[half](dst[:, :, 16 * half : 16 * half + 16], src)
                else:
                    cast[half](dst[:, 2 * half : 2 * half + 2], src[:, 2 * half : 2 * half + 2])
            for half in range(2):
                cols = slice(2 * P * half, 2 * P * (half + 1))
                nc.vector.quantize_mx(
                    out=w_codes[key][:, cols].bitcast(E4M3),
                    scales=w_scales[key][:, cols],
                    in_=grouped[:, cols, :].rearrange("p c i -> p (c i)"),
                )

        def front_of_w3(b, grouped):
            w_codes["w3", b] = keep.tile([P, PASS], U32, name="codes_w3%d" % b, align_bytes=64)
            w_scales["w3", b] = keep.tile([P, PASS], U8, name="scales_w3%d" % b, align_bytes=64)
            nc.vector.tensor_copy(
                grouped.rearrange("p (g e i) -> p g i e", e=4, i=4),
                raws["w3", b][:, :, :CHUNK].rearrange("p i (g e) -> p g i e", e=4),
            )

        def spent(b):
            if b == 0:
                return w3_back[:]
            return raws["w3", 1][:, 0:2, :CHUNK].bitcast(BF16)

        def back_piece(b, t):
            if (b, t) == (0, 1):
                return roots[3][:, :CHUNK].bitcast(BF16)
            return spent(b)[:, t, :]

        def back_of_w3(b):
            if b == 0:
                for t, cast in enumerate((nc.vector.tensor_copy, nc.scalar.copy)):
                    cast(
                        back_piece(b, t).rearrange("p (g e i) -> p g i e", e=4, i=4),
                        raws["w3", b][:, :, CHUNK + P * t : CHUNK + P * (t + 1)].rearrange("p i (g e) -> p g i e", e=4),
                    )
            else:
                nc.gpsimd.tensor_scalar(
                    spent(b).rearrange("p t (c i) -> p t c i", i=4),
                    raws["w3", b][:, :, CHUNK:].rearrange("p i (t c) -> p t c i", t=2),
                    1.0, 0.0, ALU.mult, ALU.add,
                )

        def quantize_w3(b, c0, grouped):
            cols = slice(c0, c0 + grouped.shape[1] // 4)
            nc.vector.quantize_mx(out=w_codes["w3", b][:, cols].bitcast(E4M3), scales=w_scales["w3", b][:, cols], in_=grouped)

        w3_back = keep.tile([P, 2, 2 * CHUNK], BF16, name="w3_back", align_bytes=64)
        w3_front = keep.tile([P, 8 * CHUNK], BF16, name="w3_front", align_bytes=64)

        w1_codes = [keep.tile([P, 2 * H], U8, name="w1_codes%d" % b, align_bytes=64) for b in range(2)]
        w1_dealt = keep.tile([P, 2 * H], U8, name="w1_dealt", align_bytes=64)

        def deal_codes(b):
            nc.vector.tensor_copy(
                w1_codes[b][:].bitcast(I32).rearrange("p (a t m w) -> p a m t w", a=2, t=4, w=2),
                w1_raw[b][:].bitcast(I32).rearrange("p a (m t w) -> p a m t w", t=4, w=2),
            )

        def deal_scales():
            nc.vector.tensor_copy(
                w1_dealt[:].bitcast(I32).rearrange("p (g t m) -> p g m t", g=4, t=4),
                w1_plane[:].bitcast(I32).rearrange("p a (b m t) -> p (a b) m t", b=2, t=4),
            )

        taken = {"damping": 0, "drive": 0, "change": 0}

        def next_bank(kind):
            bank = psum.tile([P, PASS], F32, name="%s%d" % (kind, taken[kind] % BANKS[kind]))
            taken[kind] = taken[kind] + 1
            return bank

        def in_word_order(bank):
            return bank[:].rearrange("p (t j) -> p j t", t=4)

        def as_words(tile):
            return tile.rearrange("p (j t) -> p j t", t=4)

        def place_of(u):
            return u // 4, u % 4 // 2, P * (u % 2)

        def entries_of(u):
            c, b, j0 = place_of(u)
            return slice(CHUNK * c + j0, CHUNK * c + j0 + P)

        sizes, roots, factors = {}, {}, {}

        def damp(u):
            b, js = place_of(u)[1], entries_of(u)
            if u in (4, 5):
                bank = next_bank("change")
            else:
                bank = psum.tile([P, PASS], F32, name="damping%d" % (u % 3 if u < 4 else 1 + u % 2))
            for a in range(2):
                for t in range(4):
                    ts = slice(P * t, P * (t + 1))
                    nc.tensor.matmul_mx(
                        out=bank[:, ts],
                        lhsT=w_codes["w2", b, a][:, ts].bitcast(E4M3),
                        lhsT_scale=w_scales["w2", b, a][:, ts],
                        rhs=v_codes[a][:, js].bitcast(E4M3),
                        rhs_scale=v_moved[:, a, js],
                        start=(a, t) == (0, 0),
                        stop=(a, t) == (1, 3),
                    )
            if u in (6, 7):
                sizes[u] = factors[u - 4]
            else:
                sizes[u] = ring.tile([P, PASS], F32, name="early_size" if u in (4, 5) else "size", bufs=2 if u in (4, 5) else 3)
            nc.scalar.activation(as_words(sizes[u][:]), in_word_order(bank), ACT.Abs)

        def root(u):
            roots[u] = ring.tile([P, PASS], F32, name="early_root" if u in (4, 5) else "root", bufs=2 if u in (4, 5) else 3, align_bytes=64)
            nc.scalar.activation(roots[u][:], sizes[u][:], ACT.Abs_reciprocal_sqrt, bias=one)

        def square(u):
            if u == 4:
                factors[u] = casts["w2", 1, 1][:, CHUNK:, :].rearrange("p c i -> p (c i)").bitcast(F32)
                nc.scalar.activation(factors[u], roots[u][:], ACT.Square)
                return
            if u == 5:
                factors[u] = keep.tile([P, PASS], F32, name="early_factor")
            else:
                factors[u] = ring.tile([P, PASS], F32, name="factor", bufs=4)
            nc.scalar.activation(factors[u][:], roots[u][:], ACT.Square)

        hosts = {(0, 0): ("w2", 1, 1)}
        h_grouped, h_parts, drives = {}, {}, {}

        def drive(u):
            c, b, j0 = place_of(u)
            js = entries_of(u)
            if (c, b) in hosts:
                host = raws[hosts[c, b]][:].rearrange("p i c -> p (i c)").bitcast(BF16)
                h_grouped[c, b] = host[:, : 4 * CHUNK]
            elif (c, b) == (1, 0):
                h_grouped[c, b] = w3_front[:, : 4 * CHUNK]
            elif j0 == 0 and c > 0:
                h_grouped[c, b] = ring.tile([P, 4 * CHUNK], BF16, name="h_grouped", align_bytes=64, bufs=4)[:]
            bank = next_bank("change" if u == 5 else "drive")
            for t in range(4):
                for a in range(2):
                    col = P * ((2 * a + b) * 4 + t)
                    nc.tensor.matmul_mx(
                        out=bank[:, P * t : P * (t + 1)],
                        lhsT=w1_codes[b][:, 2 * P * (4 * a + t) : 2 * P * (4 * a + t + 1)].bitcast(E2M1),
                        lhsT_scale=w1_dealt[:, col : col + P],
                        rhs=v_codes[a][:, js].bitcast(E4M3),
                        rhs_scale=v_moved[:, a, js],
                        start=(a == 0),
                        stop=(a == 1),
                    )
            if (c, b) == (0, 1):
                h_parts[u] = raws["w3", 1][:, u % 2, :CHUNK].bitcast(BF16)
            else:
                h_parts[u] = h_grouped[c, b][:, 4 * j0 : 4 * (j0 + P)]
            if on_gpsimd(u):
                drives[u] = ring.tile([P, PASS], F32, name="drive", bufs=2)
                nc.scalar.copy(as_words(drives[u][:]), in_word_order(bank))
            else:
                nc.vector.tensor_tensor(
                    as_words(h_parts[u]), in_word_order(bank), as_words(factors[u][:]), ALU.mult
                )

        h_codes, h_scales = {}, {}

        def quantize_h(c, b):
            h_codes[c, b] = keep.tile([P, CHUNK], U32, name="h_codes%d%d" % (c, b), align_bytes=64)
            h_scales[c, b] = keep.tile([P, CHUNK], U8, name="h_scales%d%d" % (c, b), align_bytes=64)
            if (c, b) == (0, 1):
                for u in (2, 3):
                    js = slice(P * (u % 2), P * (u % 2 + 1))
                    nc.vector.quantize_mx(out=h_codes[c, b][:, js].bitcast(E4M3), scales=h_scales[c, b][:, js], in_=h_parts[u])
                return
            nc.vector.quantize_mx(
                out=h_codes[c, b][:].bitcast(E4M3), scales=h_scales[c, b][:], in_=h_grouped[c, b]
            )

        def listed(c0, c1, n):
            return volume[n][:].indirect(offsets[:, CHUNK * c0 // 16 : CHUNK * c1 // 16])

        picked = keep.tile([P, S], F32, name="picked")
        totals = {}

        def add_change(c0, c1, n, step):
            ns = slice(P * n, P * (n + 1))
            width = CHUNK * (c1 - c0)
            bank = next_bank("change")[:, :width]
            for c in range(c0, c1):
                for b in (1, 0):
                    nc.tensor.matmul_mx(
                        out=bank[:, CHUNK * (c - c0) : CHUNK * (c - c0 + 1)],
                        lhsT=w_codes["w3", b][:, ns].bitcast(E4M3),
                        lhsT_scale=w_scales["w3", b][:, ns],
                        rhs=h_codes[c, b][:].bitcast(E4M3),
                        rhs_scale=h_scales[c, b][:],
                        start=(b == 1),
                        stop=(b == 0),
                    )
            totals[c0, n] = ring.tile([P, width], F32, name="total", bufs=2)
            if n == 0:
                nc.vector.tensor_tensor(
                    totals[c0, n][:], bank, picked[:, CHUNK * c0 : CHUNK * c1], ALU.add
                )
            else:
                if on_gpsimd(step):
                    change = h_parts[step].bitcast(F32)
                else:
                    change = ring.tile([P, width], F32, name="change", bufs=2)[:]
                nc.scalar.copy(change, bank)
                nc.vector.tensor_tensor(totals[c0, n][:], listed(c0, c1, n), change, ALU.add)

        def put_back(c0, c1, n, step):
            width = CHUNK * (c1 - c0)
            if step == LAST_UNIT:
                new = factors[step][:, :width]
            else:
                new = ring.tile([P, width], F32, name="new", bufs=2)[:]
            nc.scalar.activation(new, totals[c0, n][:], ACT.Relu)
            nc.vector.tensor_copy(listed(c0, c1, n), new)
            if c1 == CHUNKS:
                pieces = 2 if n == ROW_TILES - 1 else 1
                for i in range(pieces):
                    cols = slice(T // pieces * i, T // pieces * (i + 1))
                    nc.sync.dma_start(out[P * n : P * (n + 1), cols], volume[n][:, cols])

        last_tile = ROW_TILES - 1
        updates = [
            (c, c + 1, n)
            for c in range(CHUNKS)
            for n in range(ROW_TILES)
            if c < CHUNKS - 2 or n < last_tile
        ] + [(CHUNKS - 2, CHUNKS, last_tile)]

        on_scalar, on_vector = (nc.scalar.copy,) * 2, (nc.vector.tensor_copy,) * 2
        quantize_weight(("w2", 0, 0), "m t e", on_scalar)
        quantize_weight(("w2", 0, 1), "m t e", (nc.scalar.copy, nc.vector.tensor_copy))
        deal_scales()
        quantize_weight(("w2", 1, 0), "m t e", on_vector)
        deal_codes(0)
        quantize_weight(("w2", 1, 1), "m t e", on_vector)
        deal_codes(1)

        passes = [
            (scalar_pass, u + ahead)
            for u in range(-2, UNITS)
            for ahead, scalar_pass in ((2, damp), (1, root), (0, square))
            if 0 <= u + ahead < UNITS
        ]
        done = 0
        for step in range(FIRST_UPDATE + len(updates) + 1):
            due = 3 * step + 6
            for scalar_pass, u in passes[done:due]:
                scalar_pass(u)
            done = due
            if step == 2:
                front_of_w3(0, w3_front[:, : 4 * CHUNK])
                quantize_h(0, 0)
                quantize_w3(0, 0, w3_front[:, : 4 * CHUNK])
                front_of_w3(1, w3_front[:, 4 * CHUNK :])
            if 0 <= step < UNITS:
                drive(step)
            if step == 3:
                quantize_w3(1, 0, w3_front[:, 4 * CHUNK :])
                quantize_h(0, 1)
                nc.vector.tensor_copy(picked[:], volume[0][:].indirect(offsets[:]))
                for b in range(2):
                    back_of_w3(b)
            if step == 5:
                for b in range(2):
                    for t in range(2):
                        quantize_w3(b, CHUNK + P * t, back_piece(b, t))
            k = step - FIRST_UPDATE
            if 0 <= k < len(updates):
                add_change(*updates[k], step)
            if on_gpsimd(step):
                nc.gpsimd.tensor_tensor(h_parts[step], drives[step][:], factors[step][:], ALU.mult)
            if 3 < step < UNITS and step % 2 == 1:
                quantize_h(*place_of(step)[:2])
            if 0 < k:
                put_back(*updates[k - 1], step)
